import numpy as np, ml_dtypes
CORES = [35,38,43,46]
N = 4
BF = ml_dtypes.bfloat16
def gentries(a):
    return np.ascontiguousarray(a.reshape(8, 16, -1).transpose(0, 2, 1)).reshape(8, -1)
def gtable(e):
    e = np.asarray(e); return np.ascontiguousarray(e.reshape(8, -1, 16).transpose(0, 2, 1)).reshape(128, -1).astype(np.int32)
D, UG, B, A, NB, KG = 3, 16, 6, 2, 32, 16
U, V, E, S, K = 8 * UG, 2 ** B, 2 ** (A * B), 16 * NB, 8 * KG // N
def stored(c):
    return np.ascontiguousarray(c.reshape(N, 8, UG, NB, 16).transpose(0, 1, 4, 3, 2)).reshape(N, 128, -1).astype(np.int32)
def unstored(x):
    return np.ascontiguousarray(x.reshape(N, 8, 16, NB, UG).transpose(0, 1, 4, 3, 2)).reshape(N, U, S).astype(np.int64)
def pack(t, c, gv, wr):
    return {"tb": t.reshape(N, 8, -1).astype(np.float32).astype(BF), "x": stored(c), "give": np.stack([gtable(v.reshape(8, -1)) for v in gv]), "wires": np.stack([gtable(v.reshape(8, -1)) for v in wr])}
def draw(rng):
    return rng.integers(0, V, (N, 8, D, UG, E)), rng.integers(0, V, (N, U, S)), rng.integers(0, U, (N, 8, D, KG)), rng.integers(0, N * K, (N, 8, D, A, UG))
def setup_inputs(rng):
    return pack(*draw(rng))
def setup_inputs_ends(rng):
    t, c, gv, wr = draw(rng)
    t = rng.integers(0, 2, t.shape) * (V - 1); t[..., 0] = 0; t[..., E - 1] = V - 1; c = rng.integers(0, 2, c.shape) * (V - 1); c[:, :, 0] = 0; c[:, :, S - 1] = V - 1
    gv = rng.choice(np.array([0, UG - 1, UG, 7 * UG, U - 1]), gv.shape); wr = rng.choice(np.array([0, K - 1, K, N * K - K, N * K - 1]), wr.shape)
    return pack(t, c, gv, wr)
def setup_inputs_one(rng):
    t, c, gv, wr = draw(rng)
    gv[:] = gv[..., :1].copy(); wr[:] = wr[:, :, :, :1].copy(); q = rng.integers(0, N); wr[q] = wr[q][..., :1].copy()
    return pack(t, c, gv, wr)
def setup_inputs_next(rng):
    t, c, gv, wr = draw(rng)
    i = rng.integers(0, 2, (N, 8, D, UG, 1)) * (A - 1); t = (np.arange(E) >> (B * (A - 1 - i))) & (V - 1)
    wr = wr % K + K * ((np.arange(N) + 1) % N).reshape(N, 1, 1, 1, 1)
    return pack(t, c, gv, wr)
def setup_inputs_spread(rng):
    t, c, gv, wr = draw(rng)
    t = t >> rng.integers(0, B + 1, (N, 8, D, UG, 1)); c = c >> rng.integers(0, B + 1, (N, U, 1))
    gv = (rng.random(gv.shape) ** 3 * U).astype(np.int64); wr = (rng.random(wr.shape) ** 3 * (N * K)).astype(np.int64)
    return pack(t, c, gv, wr)
def check_inputs(d):
    bad = []
    for name, top in (("x", V), ("give", U), ("wires", N * K)):
        if not ((d[name] >= 0) & (d[name] < top)).all(): bad.append(name)
    t = d["tb"].astype(np.float32)
    if not ((t >= 0) & (t < V) & (np.floor(t) == t)).all(): bad.append("tb")
    return bad
def reference(tb, x, give, wires):
    t = tb.astype(np.float32).astype(np.int64).reshape(N, 8, D, UG, E)
    gv = np.stack([gentries(v) for v in give]).reshape(N, 8 * D * KG).reshape(N, 8, D, KG)
    wr = np.stack([gentries(v) for v in wires]).reshape(N, 8, D, A, UG)
    c = unstored(x)
    for l in range(D):
        lines = np.zeros((N, N * K, S), np.int64); new = np.zeros((N, U, S), np.int64)
        for q in range(N):
            lines[:, q * K:(q + 1) * K] = c[q][gv[q, :, l].reshape(-1)].reshape(N, K, S)
        for r in range(N):
            a = np.zeros((8, UG, S), np.int64)
            for i in range(A):
                a = a * V + lines[r][wr[r, :, l, i]]
            new[r] = np.take_along_axis(t[r, :, l], a, axis=2).reshape(U, S)
        c = new
    return {"y": np.asarray(stored(c), np.float32)}

@@ -1,0 +1,400 @@
+from concourse.bass import DstId, RemoteDMATransfer
+from concourse.mybir import AluOpType, ActivationFunctionType
+
+OP = AluOpType
+COPY = ActivationFunctionType.Copy
+NBLK = 4
+NT = 3 * NBLK
+A4 = [[0], [1], [2], [3]]
+MODE = "BAA"
+SENDS = {0: [[0], [1, 2, 3]], 1: A4, 2: A4}
+CYC, PEC, GAT, FIX, WAKE, REM, DMA = 1.0e-3, 0.5e-3, 1.56e-3, 0.05, 0.06, 3.5, 2.0
+TQ = {1: 4, 2: 3}
+NV = [54, 50, 60, 64, 58, 56, 62, 60, 50, 54, 56]
+V0 = [44, 40, 42, 50, 48, 52, 54, 46, 40, 50, 50]
+EXTRA = {1: {"v": ["gb", "og1"]}, 2: {"v": ["og2"], "p": ["wm1"]}, 3: {"s": ["wc1"]}, 4: {"p": ["wm2"]}, 6: {"s": ["wc2"]}}
+
+
+def pieces(t):
+    if t == NT - 1:
+        return [(0, 64, [("v", 0, 42), ("s", 42, 22)]), (64, 64, [("v", 64, 28), ("s", 92, 36)])]
+    n = NV[t]
+    return [(0, n, [("v", 0, V0[t]), ("v", V0[t], n - V0[t])]), (n, 128 - n, [("s", n, 128 - n)])]
+
+
+def steps(then, t):
+    early = [(t + 1, "lt")] if t == 0 else []
+    then("v", (t, "gv0"), (t, "xv"), (t - 1, "pms"), *early, (t, "gv1"), (t + 1, "off"), (t - 1, "z"), (t + 2, "lt"))
+    then("s", (t, "xs"), (t, "gs0"), (t, "gs1"))
+    early = [(t + 1, "tr")] if t == 0 else []
+    then("p", (t - 1, "m1"), *early, (t + 1, "a"), (t + 2, "tr"), (t, "xp"), (t - 1, "otr"), (t, "m0"))
+
+
+SCRATCH = {
+    "xi": ("sbuf", [128, 512], "int32"),
+    "gi": ("sbuf", [128, 3], "int32"),
+    "gd": ("dram", [4, 128, 3], "int32"),
+    "gg": ("sbuf", [128, 3], "int32"),
+    "wi": ("sbuf", [128, 6], "int32"),
+    "tab": ("sbuf", [128, 3, 4096], "bfloat16"),
+    "jc": ("sbuf", [128, 128], "bfloat16"),
+    "jl": ("sbuf", [128, 128], "bfloat16"),
+    "jr": ("sbuf", [128, 128], "bfloat16"),
+    "pint": ("sbuf", [128, 4], "int32"),
+    "pf": ("sbuf", [128, 1], "float32"),
+    "plow": ("sbuf", [128, 1], "float32"),
+    "m16": ("sbuf", [128, 16], "float32"),
+    "ident": ("sbuf", [128, 128], "bfloat16"),
+    "id4": ("sbuf", [128, 4, 2, 16], "bfloat16"),
+    "pall": ("sbuf", [128, 2, 2, 4, 2, 16], "bfloat16"),
+    "ones": ("sbuf", [128, 128], "bfloat16"),
+    "msk": ("sbuf", [128, 16, 128], "bfloat16"),
+    "gl": ("sbuf", [128, 3], "float32"),
+    "gbs": ("sbuf", [128, 3], "float32"),
+    "og": ("sbuf", [128, 3, 128], "bfloat16"),
+    "dg": ("sbuf", [128, 128], "bfloat16"),
+    "one": ("sbuf", [128, 128], "bfloat16"),
+    "wf": ("sbuf", [128, 6], "float32"),
+    "oh": ("sbuf", [128, 6, 128], "bfloat16"),
+    "wm": ("sbuf", [128, 3, 128], "bfloat16"),
+    "wc": ("sbuf", [128, 3, 4, 128], "bfloat16"),
+    "xb": ("sbuf", [128, 512], "bfloat16"),
+    "xt": ("sbuf", [128, NBLK, 4, 2, 16], "bfloat16"),
+    "cu": ("sbuf", [128, NBLK, 128], "bfloat16"),
+    "lt": ("sbuf", [128, NT, 128], "bfloat16"),
+    "off": ("sbuf", [128, NT, 128], "uint16"),
+    "gt": ("sbuf", [128, NT, 2048], "bfloat16"),
+    "pms": ("sbuf", [128, NBLK, 4, 2, 16], "bfloat16"),
+    "yo": ("sbuf", [128, 512], "float32"),
+    "q1": ("psum", [128, 16, 2, 16], "float32"),
+    "pm0": ("psum", [128, 512], "float32"),
+    "pm1": ("psum", [128, 512], "float32"),
+    "pa": ("psum", [128, 512], "float32"),
+    "pw": ("psum", [128, 512], "float32"),
+    "pv": ("psum", [128, 512], "float32"),
+    "pl": ("psum", [128, 512], "float32"),
+    "pr": ("psum", [128, 8, 128], "bfloat16"),
+}
+SEMAPHORES = ["v", "p", "s", "k", "x0", "x1", "gs", "gd", "gg", "ga", "wl", "yd", "loc"]
+SEMAPHORES += ["t%d%d" % (_l, _q) for _l in range(3) for _q in range(4)]
+for _e in SENDS:
+    for _c in range(len(SENDS[_e])):
+        SCRATCH["z%d_%d" % (_e, _c)] = ("sbuf", [128, 4 if MODE[_e] == "A" else 7, len(SENDS[_e][_c]), 128 if MODE[_e] == "A" else 32], "bfloat16")
+        SEMAPHORES.append("a%d_%d" % (_e, _c))
+
+
+def layout(nodes):
+    users = [[] for _ in nodes]
+    for n in nodes:
+        for d in n["deps"]:
+            users[d["i"]].append(n)
+    for n in reversed(nodes):
+        n["cp"] = min(n["dur"].values()) + n["lat"] + max([WAKE + u["cp"] for u in users[n["i"]]] + [0.0])
+    free = {"v": 0.0, "p": 0.0, "s": 0.0, "k": 0.0, "y": 0.0}
+    left = list(nodes)
+    order = []
+    while left:
+        best = None
+        for q in sorted(free):
+            cand = []
+            for n in left:
+                if q in n["dur"] and (n.get("prev") is None or "end" in n["prev"]) and all("end" in d for d in n["deps"]):
+                    cand.append((max([d["end"] + WAKE for d in n["deps"]] + [0.0]), n))
+            if not cand:
+                continue
+            t0 = max(free[q], min(c[0] for c in cand))
+            t, n = min([(-c[1]["cp"] - c[1].get("pri", 0.0), c[1]["i"], max(t0, c[0]), c[1]) for c in cand if c[0] <= t0])[2:]
+            key = (t, t + n["dur"][q], n["i"])
+            if best is None or key < best[0]:
+                best = (key, q, n)
+        (t, e, _), q, n = best
+        n["q"], n["start"], n["end"] = q, t, e + n["lat"]
+        free[q] = e
+        left.remove(n)
+        order.append(n)
+    return order
+
+
+def rank_program(g, core, T, topo):
+    r = T.rank_of(core)
+    if r is None:
+        return
+    cores = T.cores
+    queues = {"v": g.vector, "p": g.tensor, "s": g.scalar, "k": g, "y": g.sync}
+    nodes = []
+
+    def node(dur, deps, emit, sem=None, n=1, lat=0.0):
+        flat = []
+        for d in deps:
+            if isinstance(d, list):
+                flat += [x for x in d if x is not None]
+            elif d is not None:
+                flat.append(d)
+        x = {"i": len(nodes), "dur": dur, "deps": flat, "emit": emit, "sem": sem, "n": n, "lat": lat}
+        nodes.append(x)
+        return x
+
+    def V(deps, name, *a, cy=64):
+        f = {"copy": g.vector.tensor_copy, "ts": g.vector.tensor_scalar, "tr": g.vector.transpose,
+             "set": g.vector.memset}[name]
+        return node({"v": FIX + max(cy, 64) * CYC}, deps, lambda q: f(*a))
+
+    def VS(deps, out, in_, vcy, scy, on="vs"):
+        def emit(q):
+            if q == "v":
+                return g.vector.tensor_copy(out, in_)
+            return g.scalar.activation(out, in_, COPY)
+        dur = {"v": FIX + vcy * CYC, "s": FIX + 0.015 + scy * CYC}
+        return node({q: dur[q] for q in on}, deps, emit)
+
+    def scaled(deps, out, in_, col):
+        def emit(q):
+            if q == "v":
+                return g.vector.tensor_scalar(out, in_, col, None, OP.mult)
+            return g.scalar.activation(out, in_, COPY, scale=col)
+        return node({"v": FIX + 64 * CYC, "s": FIX + 0.015 + 128 * CYC}, deps, emit)
+
+    def MM(deps, calls):
+        def emit(q):
+            for out, lhs, rhs, st, sp, cy in calls:
+                x = g.tensor.matmul(out, lhs, rhs, st, sp)
+            return x
+        return node({"p": 0.02 + sum([c[5] for c in calls]) * PEC}, deps, emit)
+
+    def TR(deps, calls):
+        def emit(q):
+            for out, in_ in calls:
+                x = g.tensor.transpose(out, in_, T.ident[:])
+            return x
+        return node({"p": 0.02 + 128 * PEC * len(calls)}, deps, emit)
+
+    def dma(q, deps, out, in_, s, more=0.0, pri=0.0):
+        x = node({q: 0.05}, deps, lambda qq: queues[qq].dma_start(out, in_), s, 16, DMA + more)
+        x["pri"] = pri
+        return x
+
+    def iota(out, n, pattern, base, cm):
+        return node({"k": 0.13 + 2 * n * CYC}, [], lambda q: g.iota(out, pattern, base, cm, allow_small_or_imprecise_dtypes=True))
+
+    d_gd = dma("s", [], T.gd[0], T.give[:], "gd")
+    d_give = dma("s", [], T.gi[:], T.give[:], "gs")
+    d_x = [dma("y", [], T.xi[:, 256 * h:256 * h + 256], T.x[:, 256 * h:256 * h + 256], "x%d" % h, 0.1 * h) for h in range(2)]
+    d_wire = dma("s", [], T.wi[:], T.wires[:], "wl")
+    tabs = [[], [], []]
+
+    def load_table(l, h, n, more, deps=()):
+        tabs[l].append(dma("y", list(deps), T.tab[16 * h:16 * h + 16 * n, l, :], T.tb[h:h + n, l * 65536:(l + 1) * 65536],
+                           "t%d%d" % (l, h // n % 4), more, -1000.0))
+
+    for h in (0, 2, 4):
+        load_table(0, h, 2, 1.5 + 0.4 * h)
+
+    s0 = 32 if r % 2 == 0 else -32
+    s1 = 64 if r < 2 else -64
+    k_pint = node({"k": 0.13}, [], lambda q: g.iota(T.pint[:, 0:1], [[0, 1]], 0, 1))
+    k_pf = iota(T.pf[:], 1, [[0, 1]], 0, 1)
+    k_jc = iota(T.jc[:], 128, [[1, 128]], 0, 0)
+    k_jl = iota(T.jl[:], 128, [[-s1, 2], [-s0, 2], [1, 32]], 32 * (r ^ 3), 0)
+    k_jr = iota(T.jr[:], 128, [[s1, 2], [s0, 2], [1, 32]], 32 * r, 0)
+    c_pz = V([], "set", T.pall[:], 0.0, cy=256)
+    c_ones = V([], "set", T.ones[:], 1.0)
+    c_lo = V([k_pint], "ts", T.pint[:, 2:3], T.pint[:, 0:1], 15, None, OP.bitwise_and)
+    c_low = V([c_lo], "copy", T.plow[:], T.pint[:, 2:3])
+    c_id = V([k_jc, k_pf], "ts", T.ident[:], T.jc[:], T.pf[:], None, OP.is_equal)
+    c_id4 = V([k_jc, k_pf], "ts", T.id4[:], T.jc[:], T.pf[:], None, OP.is_equal)
+    c_m16 = V([k_jc, c_low], "ts", T.m16[:], T.jc[:, 0:16], T.plow[:], None, OP.is_equal)
+    c_pall = []
+    for x2 in range(2):
+        for g2 in range(2):
+            c_pall.append(V([c_id4, c_pz], "copy", T.pall[:, x2, g2, :, x2, :], T.id4[:, :, g2, :]))
+
+    dst = {d: cores[r ^ d] for d in (1, 2, 3)}
+    far = [d for d in dst if topo.chip(dst[d]) != topo.chip(core)]
+    near = [d for d in dst if d not in far]
+    use = {}
+    farset = set()
+    for j, d in enumerate(far):
+        en = topo.engines(core, dst[d])
+        farset |= set(en)
+        w = len(en) // len(far)
+        use[d] = en[j * w:j * w + w]
+    for j, d in enumerate(near):
+        en = [x for x in topo.engines(core, dst[d]) if x not in farset]
+        w = len(en) // len(near)
+        use[d] = en[j * w:j * w + w]
+    total_eng = sum(len(use[d]) for d in dst)
+
+    def send(deps, name, src, dest):
+        def emit(q):
+            tr = []
+            for d in (1, 2, 3):
+                rid, pid, _ = topo.addr(dst[d])
+                tr.append(RemoteDMATransfer(dst_ids=[DstId(rid=rid, pnc=pid)], dma_engine_mask=sum(1 << x for x in use[d]),
+                                            remote_sem=T.sem[name], src=src(d), dst=dest(d)))
+            g.remote_dma_fused(tr, local_sem=T.sem.loc)
+            return None
+        return node({"k": 0.6}, deps, emit, name, total_eng, REM - 0.6)
+
+    arr, own = {}, {}
+    free = {"pr": None, "pl": None, "pw": None, "pv": None, "pa": None, "pm0": None, "pm1": None, "q1": None}
+    a_give = send([d_gd], "ga", lambda d: T.gd[0], lambda d: T.gd[d])
+
+    xb, xt = [], []
+    for k in range(NBLK):
+        xb.append(V([d_x[k // 2]], "copy", T.xb[:, 128 * k:128 * k + 128], T.xi[:, 128 * k:128 * k + 128], cy=128))
+        xt.append(V([xb[k]], "tr", T.xt[:, k], T.xb[:, 128 * k:128 * k + 128]))
+
+    c_gl = V([d_give], "copy", T.gl[:], T.gi[:])
+    c_dg = V([c_gl, k_jr, k_pf], "ts", T.dg[:], T.jr[:], T.pf[:], T.gl[:, 0:1], OP.is_equal, OP.mult)
+    a = MM([c_dg, c_ones], [(T.pw[:, 0:128], T.ones[:], T.dg[:], True, True, 128)])
+    free["pw"] = c_one = V([a, k_pf], "ts", T.one[:], T.pw[:, 0:128], T.pf[:], None, OP.is_equal, cy=128)
+
+    def zslot(e, k):
+        for ci, blks in enumerate(SENDS[e]):
+            if k in blks:
+                return T["z%d_%d" % (e, ci)], "a%d_%d" % (e, ci), blks.index(k), blks
+
+    def post(e, k, deps, src, on):
+        z, name, i, blks = zslot(e, k)
+        if MODE[e] == "A":
+            own[(e, k)] = c = VS(deps, z[:, 3, i, :], src, 128, 128, on)
+        else:
+            c = VS(deps, T.cu[:, k, :], src, 128, 128, on)
+            a = MM([c, c_one, free["pl"]], [(T.pl[:, 0:128], T.cu[:, k, :], T.one[:], True, True, 128)])
+            free["pl"] = own[(e, k)] = VS([a], z[:, 3:7, i, :], T.pl[:, 0:128], 128, 128)
+        if k == blks[-1]:
+            n = send([own[(e, b)] for b in blks], name, lambda d: z[:, 3 if MODE[e] == "A" else 3 + d, :, :], lambda d: z[:, 3 - d, :, :])
+            for b in blks:
+                arr[(e, b)] = n
+        return c
+
+    for k in range(NBLK):
+        a = MM([xt[k], c_pall, free["q1"]], [(T.q1[:, 0:4, bp, :], T.pall[:, g2, bp], T.xt[:, k, :, g2, :], g2 == 0, g2 == 1, 64)
+                                             for bp in range(2) for g2 in range(2)])
+        free["q1"] = post(0, k, [a], T.q1[:, 0:4], "s" if k == 0 else "vs")
+    load_table(0, 6, 2, 2.5, [own[(0, 1)]])
+
+    X = {}
+    d_gg = [dma("y", [a_give if j < 3 else None], T.gg[32 * j:32 * j + 32, :],
+                T.gd[3 - j, 32 * r:32 * r + 32, :] if j < 3 else T.give[32 * r:32 * r + 32, :], "gg", 0.0, -500.0) for j in (3, 0, 1, 2)]
+    c_gb = X["gb"] = V([d_gg], "copy", T.gbs[:], T.gg[:])
+    c_wf = V([d_wire], "copy", T.wf[:], T.wi[:])
+    c_w = []
+    for l in range(3):
+        o0 = V([c_wf, k_jl], "ts", T.oh[:, 2 * l, :], T.jl[:], T.wf[:, 2 * l:2 * l + 1], 64.0, OP.is_equal, OP.mult)
+        o1 = V([c_wf, k_jl], "ts", T.oh[:, 2 * l + 1, :], T.jl[:], T.wf[:, 2 * l + 1:2 * l + 2], None, OP.is_equal)
+        b = ["pm1", "pm0", "pa"][l]
+        a = MM([o0, o1, c_id, free[b]], [(T[b][:, 0:128], T.oh[:, 2 * l, :], T.ident[:], True, False, 128),
+                                         (T[b][:, 0:128], T.oh[:, 2 * l + 1, :], T.ident[:], False, True, 128)])
+        free[b] = c_wm = VS([a], T.wm[:, l, :], T[b][:, 0:128], 128, 128)
+        if MODE[l] == "B":
+            c_w.append([c_wm])
+            continue
+        c_og = X["og%d" % l] = V([c_gb, k_jc], "ts", T.og[:, l, :], T.jc[:], T.gbs[:, l:l + 1], None, OP.is_equal)
+        b = ["pw", "pv"][l % 2]
+        X["wm%d" % l] = []
+        a = free[b]
+        for j in range(4):
+            a = MM([c_wm, c_og, a], [(T[b][:, 128 * j:128 * j + 128], T.og[32 * j:32 * j + 32, l, :], T.wm[32 * j:32 * j + 32, l, :], True, True, 128)])
+            X["wm%d" % l].append(a)
+        free[b] = X["wc%d" % l] = VS([a], T.wc[:, l, :, :], T[b][:, 0:512], 512, 512, "s")
+        c_w.append([free[b]])
+    c_msk = [scaled([c_m16, c_id], T.msk[:, u, :], T.ident[:], T.m16[:, u:u + 1]) for u in range(16)]
+
+    B = []
+    for t in range(NT):
+        l, k = divmod(t, NBLK)
+        pm = "pm%d" % (t % 2)
+        o = {}
+        B.append(o)
+        for q in EXTRA.get(t, {}):
+            o["x" + q] = []
+            for n in EXTRA[t][q]:
+                o["x" + q] += X[n] if isinstance(X[n], list) else [X[n]]
+        z, _, i, blks = zslot(l, k)
+        if MODE[l] == "A":
+            o["a"] = MM([arr[(l, k)], own[(l, k)], c_w[l], free["pa"]],
+                        [(T.pa[:, 0:128], T.wc[:, l, j, :], z[:, j, i, :], j == 3, j == 2, 128) for j in (3, 0, 1, 2)])
+        else:
+            o["tr"] = TR([arr[(l, k)], own[(l, k)], free["pr"], c_id],
+                         [(T.pr[:, 0, :], z[:, 0:4, 0, :])] if len(blks) == 1 else [(T.pr[32 * j:32 * j + 32, 0, :], z[:, j, i, :]) for j in range(4)])
+            o["lt"] = free["pr"] = VS([o["tr"]], T.lt[:, t, :], T.pr[:, 0, :], 64, 128, "v")
+            o["a"] = MM([o["lt"], c_w[l], free["pa"]], [(T.pa[:, 0:128], T.wm[:, l, :], T.lt[:, t, :], True, True, 128)])
+        o["off"] = free["pa"] = V([o["a"]], "copy", T.off[:, t, :], T.pa[:, 0:128], cy=128)
+        if t == 0:
+            for l2 in (1, 2):
+                for h in range(8):
+                    load_table(l2, h, 1, 0.6, [arr[(0, 0)] if l2 == 1 and h < TQ[1] else (tabs[1] + tabs[2])[-TQ[l2]]])
+
+        def gather(q, b, n):
+            x = VS([o["off"], tabs[l]], T.gt[:, t, 16 * b:16 * b + 16 * n], T.tab[:, l, :].indirect(T.off[:, t, b:b + n]),
+                   16 * n * GAT / CYC, 16 * n * GAT / CYC, q)
+            j = 1 if "g%s0" % q in o else 0
+            o["g%s%d" % (q, j)] = x
+            return x
+
+        ms = []
+        for h, (lo, w, calls) in enumerate(pieces(t)):
+            gs = [gather(q, b, n) for q, b, n in calls]
+            o["m%d" % h] = MM([gs, free[pm], c_msk],
+                              [(T[pm][:, lo:lo + w], T.msk[:, u, :], T.gt[:, t, 16 * lo + u:16 * lo + 16 * w:16], u == 0, u == 15, max(64, w))
+                               for u in range(16)])
+            ms.append(o["m%d" % h])
+        if l < 2:
+            o["pms"] = free[pm] = post(l + 1, k, ms, T[pm][:, 0:128], "v")
+        else:
+            o["pms"] = free[pm] = VS(ms, T.pms[:, k], T[pm][:, 0:128], 128, 128, "v")
+            o["otr"] = MM([o["pms"], free["q1"], c_pall], [(T.q1[:, 0:4, g2, :], T.pall[:, x2, g2], T.pms[:, k, :, x2, :], x2 == 0, x2 == 1, 64)
+                                                           for g2 in range(2) for x2 in range(2)])
+            o["z"] = free["q1"] = V([o["otr"]], "tr", T.yo[:, 128 * k:128 * k + 128], T.q1[:, 0:4], cy=128)
+            dma("y", [o["z"]], T.y[:, 128 * k:128 * k + 128], T.yo[:, 128 * k:128 * k + 128], "yd")
+    last = {}
+
+    def then(q, *names):
+        for t, name in names:
+            if 0 <= t < NT and name in B[t]:
+                x = B[t][name]
+                for n in (x if isinstance(x, list) else [x]):
+                    if q in n["dur"]:
+                        n["prev"] = last.get(q)
+                        last[q] = n
+
+    way = [c_gl, xb[0], c_dg, xt[0], c_one, xb[1]]
+    for n, p in zip(way[1:], way):
+        n["prev"] = p
+    for n in c_msk:
+        n["prev"] = own[(0, 0)]
+    then("v", (0, "lt"), (0, "off"))
+    then("p", (0, "tr"), (0, "a"))
+    for t in range(NT + 1):
+        steps(then, t)
+
+    order = layout(nodes)
+    total = {}
+    for n in order:
+        s = n["sem"] or n["q"]
+        total[s] = total.get(s, 0) + n["n"]
+        n["tok"] = (s, total[s])
+    waited = {}
+
+    def wait(q, s, val):
+        if waited.get((q, s), 0) < val:
+            queues[q].wait_ge(T.sem[s], val)
+            waited[(q, s)] = val
+
+    sent = 0
+    for n in order:
+        need = {}
+        for d in n["deps"]:
+            s, val = d["tok"]
+            need[s] = max(need.get(s, 0), val)
+        for s in sorted(need):
+            wait(n["q"], s, need[s])
+        x = n["emit"](n["q"])
+        if x is None:
+            sent += n["n"]
+        else:
+            x.then_inc(T.sem[n["tok"][0]], n["n"])
+    for s in sorted(total):
+        wait("y", s, total[s])
+    wait("y", "loc", sent)

@@ -3,212 +3,112 @@ from concourse.mybir import AluOpType, ActivationFunctionType
 
 OP = AluOpType
 COPY = ActivationFunctionType.Copy
+N = 4
 NBLK = 4
 NT = 3 * NBLK
-A4 = [[0], [1], [2], [3]]
-MODE = "BAA"
-SENDS = {0: [[0], [1, 2, 3]], 1: A4, 2: A4}
-CYC, PEC, GAT, FIX, WAKE, REM, DMA = 1.0e-3, 0.5e-3, 1.56e-3, 0.05, 0.06, 3.5, 2.0
-TQ = {1: 4, 2: 3}
-NV = [54, 50, 60, 64, 58, 56, 62, 60, 50, 54, 56]
-V0 = [44, 40, 42, 50, 48, 52, 54, 46, 40, 50, 50]
-EXTRA = {1: {"v": ["gb", "og1"]}, 2: {"v": ["og2"], "p": ["wm1"]}, 3: {"s": ["wc1"]}, 4: {"p": ["wm2"]}, 6: {"s": ["wc2"]}}
-
-
-def pieces(t):
-    if t == NT - 1:
-        return [(0, 64, [("v", 0, 42), ("s", 42, 22)]), (64, 64, [("v", 64, 28), ("s", 92, 36)])]
-    n = NV[t]
-    return [(0, n, [("v", 0, V0[t]), ("v", V0[t], n - V0[t])]), (n, 128 - n, [("s", n, 128 - n)])]
-
-
-def steps(then, t):
-    early = [(t + 1, "lt")] if t == 0 else []
-    then("v", (t, "gv0"), (t, "xv"), (t - 1, "pms"), *early, (t, "gv1"), (t + 1, "off"), (t - 1, "z"), (t + 2, "lt"))
-    then("s", (t, "xs"), (t, "gs0"), (t, "gs1"))
-    early = [(t + 1, "tr")] if t == 0 else []
-    then("p", (t - 1, "m1"), *early, (t + 1, "a"), (t + 2, "tr"), (t, "xp"), (t - 1, "otr"), (t, "m0"))
-
+BASE, SPAN = [0, 8, 12, 16], [4, 12, 12, 12]
+EARLY = 6
+TQ = 4
+NEAR = 8
+VSEQ = [
+    [44, "lt1", 10, "off1", 6],
+    [40, "pms0", "lt2", "gb", "off2", 8],
+    [44, "pms1", "og1", "off3", 8, "og2"],
+    [44, "pms2", 12, "off4", 6],
+    [44, "pms3", 8, "off5", 6],
+    [44, "pms4", 8, "off6", 6],
+    [44, "pms5", 12, "off7", 6],
+    [44, "pms6", 8, "off8", 6],
+    [44, "pms7", 8, "off9", 6],
+    [30, "off10", 28, "z8"],
+    [30, "off11", 28, "z9"],
+]
+SX = {3: ["wc1"], 6: ["wc2"]}
+PX = {2: ["pw1"], 4: ["pw2"]}
+LAST = [("v", 0, 36), ("s", 36, 28), ("v", 64, 22), ("s", 86, 42)]
 
 SCRATCH = {
-    "xi": ("sbuf", [128, 512], "int32"),
+    "xi0": ("sbuf", [128, 2, 64], "int32"),
+    "xi1": ("sbuf", [128, 2, 192], "int32"),
     "gi": ("sbuf", [128, 3], "int32"),
     "gd": ("dram", [4, 128, 3], "int32"),
     "gg": ("sbuf", [128, 3], "int32"),
     "wi": ("sbuf", [128, 6], "int32"),
-    "tab": ("sbuf", [128, 3, 4096], "bfloat16"),
+    "tab": ("sbuf", [128, 2, 4096], "bfloat16"),
+    "tab3": ("sbuf", [128, 8192], "bfloat16"),
     "jc": ("sbuf", [128, 128], "bfloat16"),
-    "jl": ("sbuf", [128, 128], "bfloat16"),
-    "jr": ("sbuf", [128, 128], "bfloat16"),
-    "pint": ("sbuf", [128, 4], "int32"),
+    "jp": ("sbuf", [128, 128], "bfloat16"),
+    "jm": ("sbuf", [128, 128], "bfloat16"),
     "pf": ("sbuf", [128, 1], "float32"),
-    "plow": ("sbuf", [128, 1], "float32"),
-    "m16": ("sbuf", [128, 16], "float32"),
     "ident": ("sbuf", [128, 128], "bfloat16"),
     "id4": ("sbuf", [128, 4, 2, 16], "bfloat16"),
-    "pall": ("sbuf", [128, 2, 2, 4, 2, 16], "bfloat16"),
-    "ones": ("sbuf", [128, 128], "bfloat16"),
-    "msk": ("sbuf", [128, 16, 128], "bfloat16"),
+    "big": ("sbuf", [128, 64], "bfloat16"),
+    "msk": ("sbuf", [128, 16, 144], "bfloat16"),
     "gl": ("sbuf", [128, 3], "float32"),
     "gbs": ("sbuf", [128, 3], "float32"),
     "og": ("sbuf", [128, 3, 128], "bfloat16"),
-    "dg": ("sbuf", [128, 128], "bfloat16"),
     "one": ("sbuf", [128, 128], "bfloat16"),
     "wf": ("sbuf", [128, 6], "float32"),
     "oh": ("sbuf", [128, 6, 128], "bfloat16"),
     "wm": ("sbuf", [128, 3, 128], "bfloat16"),
-    "wc": ("sbuf", [128, 3, 4, 128], "bfloat16"),
-    "xb": ("sbuf", [128, 512], "bfloat16"),
-    "xt": ("sbuf", [128, NBLK, 4, 2, 16], "bfloat16"),
-    "cu": ("sbuf", [128, NBLK, 128], "bfloat16"),
-    "lt": ("sbuf", [128, NT, 128], "bfloat16"),
+    "wc": ("sbuf", [128, 4, 128], "bfloat16"),
+    "wz": ("sbuf", [128, 8, 9, 16], "bfloat16"),
+    "xb0": ("sbuf", [128, 4, 2, 16], "bfloat16"),
+    "xb1": ("sbuf", [128, 12, 2, 16], "bfloat16"),
+    "xt0": ("sbuf", [128, 128], "bfloat16"),
+    "xt1": ("sbuf", [128, 384], "bfloat16"),
+    "zb0": ("sbuf", [128, 7, 32], "bfloat16"),
+    "zb1": ("sbuf", [128, 7, 3, 32], "bfloat16"),
+    "lt": ("sbuf", [128, NBLK, 64, 2], "bfloat16"),
+    "z": ("sbuf", [128, 8, 4, 4, 2, 16], "bfloat16"),
     "off": ("sbuf", [128, NT, 128], "uint16"),
     "gt": ("sbuf", [128, NT, 2048], "bfloat16"),
-    "pms": ("sbuf", [128, NBLK, 4, 2, 16], "bfloat16"),
-    "yo": ("sbuf", [128, 512], "float32"),
-    "q1": ("psum", [128, 16, 2, 16], "float32"),
+    "yo": ("sbuf", [128, NBLK, 128], "float32"),
     "pm0": ("psum", [128, 512], "float32"),
     "pm1": ("psum", [128, 512], "float32"),
-    "pa": ("psum", [128, 512], "float32"),
+    "pa0": ("psum", [128, 16, 2, 16], "float32"),
+    "pa1": ("psum", [128, 16, 2, 16], "float32"),
     "pw": ("psum", [128, 512], "float32"),
-    "pv": ("psum", [128, 512], "float32"),
     "pl": ("psum", [128, 512], "float32"),
+    "pv": ("psum", [128, 4, 4, 32], "float32"),
     "pr": ("psum", [128, 8, 128], "bfloat16"),
 }
-SEMAPHORES = ["v", "p", "s", "k", "x0", "x1", "gs", "gd", "gg", "ga", "wl", "yd", "loc"]
-SEMAPHORES += ["t%d%d" % (_l, _q) for _l in range(3) for _q in range(4)]
-for _e in SENDS:
-    for _c in range(len(SENDS[_e])):
-        SCRATCH["z%d_%d" % (_e, _c)] = ("sbuf", [128, 4 if MODE[_e] == "A" else 7, len(SENDS[_e][_c]), 128 if MODE[_e] == "A" else 32], "bfloat16")
-        SEMAPHORES.append("a%d_%d" % (_e, _c))
-
-
-def layout(nodes):
-    users = [[] for _ in nodes]
-    for n in nodes:
-        for d in n["deps"]:
-            users[d["i"]].append(n)
-    for n in reversed(nodes):
-        n["cp"] = min(n["dur"].values()) + n["lat"] + max([WAKE + u["cp"] for u in users[n["i"]]] + [0.0])
-    free = {"v": 0.0, "p": 0.0, "s": 0.0, "k": 0.0, "y": 0.0}
-    left = list(nodes)
-    order = []
-    while left:
-        best = None
-        for q in sorted(free):
-            cand = []
-            for n in left:
-                if q in n["dur"] and (n.get("prev") is None or "end" in n["prev"]) and all("end" in d for d in n["deps"]):
-                    cand.append((max([d["end"] + WAKE for d in n["deps"]] + [0.0]), n))
-            if not cand:
-                continue
-            t0 = max(free[q], min(c[0] for c in cand))
-            t, n = min([(-c[1]["cp"] - c[1].get("pri", 0.0), c[1]["i"], max(t0, c[0]), c[1]) for c in cand if c[0] <= t0])[2:]
-            key = (t, t + n["dur"][q], n["i"])
-            if best is None or key < best[0]:
-                best = (key, q, n)
-        (t, e, _), q, n = best
-        n["q"], n["start"], n["end"] = q, t, e + n["lat"]
-        free[q] = e
-        left.remove(n)
-        order.append(n)
-    return order
+SEMAPHORES = ["v", "p", "s", "k", "x0", "x1", "gs", "gd", "gg", "ga", "wl", "yd", "loc", "b0", "b1", "t0"]
+SEMAPHORES += ["t%d%d" % (_l, _q) for _l in (1, 2) for _q in range(4)] + ["a%d" % _t for _t in range(8)]
 
 
 def rank_program(g, core, T, topo):
     r = T.rank_of(core)
     if r is None:
         return
-    cores = T.cores
     queues = {"v": g.vector, "p": g.tensor, "s": g.scalar, "k": g, "y": g.sync}
-    nodes = []
+    steps = {}
 
-    def node(dur, deps, emit, sem=None, n=1, lat=0.0):
-        flat = []
-        for d in deps:
-            if isinstance(d, list):
-                flat += [x for x in d if x is not None]
-            elif d is not None:
-                flat.append(d)
-        x = {"i": len(nodes), "dur": dur, "deps": flat, "emit": emit, "sem": sem, "n": n, "lat": lat}
-        nodes.append(x)
-        return x
+    def step(name, q, deps, emit, sem=None, n=1):
+        steps[name] = {"q": q, "deps": [d for d in deps if d], "emit": emit, "sem": sem or q, "n": n}
+        return name
 
-    def V(deps, name, *a, cy=64):
-        f = {"copy": g.vector.tensor_copy, "ts": g.vector.tensor_scalar, "tr": g.vector.transpose,
-             "set": g.vector.memset}[name]
-        return node({"v": FIX + max(cy, 64) * CYC}, deps, lambda q: f(*a))
+    def V(name, deps, call, *a):
+        f = {"copy": g.vector.tensor_copy, "ts": g.vector.tensor_scalar, "tr": g.vector.transpose, "set": g.vector.memset}[call]
+        return step(name, "v", deps, lambda: f(*a))
 
-    def VS(deps, out, in_, vcy, scy, on="vs"):
-        def emit(q):
-            if q == "v":
-                return g.vector.tensor_copy(out, in_)
-            return g.scalar.activation(out, in_, COPY)
-        dur = {"v": FIX + vcy * CYC, "s": FIX + 0.015 + scy * CYC}
-        return node({q: dur[q] for q in on}, deps, emit)
+    def S(name, deps, out, in_):
+        return step(name, "s", deps, lambda: g.scalar.activation(out, in_, COPY))
 
-    def scaled(deps, out, in_, col):
-        def emit(q):
-            if q == "v":
-                return g.vector.tensor_scalar(out, in_, col, None, OP.mult)
-            return g.scalar.activation(out, in_, COPY, scale=col)
-        return node({"v": FIX + 64 * CYC, "s": FIX + 0.015 + 128 * CYC}, deps, emit)
-
-    def MM(deps, calls):
-        def emit(q):
-            for out, lhs, rhs, st, sp, cy in calls:
-                x = g.tensor.matmul(out, lhs, rhs, st, sp)
+    def MM(name, deps, calls):
+        def emit():
+            for c in calls:
+                x = g.tensor.matmul(*c) if len(c) == 5 else g.tensor.transpose(c[0], c[1], T.ident[:])
             return x
-        return node({"p": 0.02 + sum([c[5] for c in calls]) * PEC}, deps, emit)
+        return step(name, "p", deps, emit)
 
-    def TR(deps, calls):
-        def emit(q):
-            for out, in_ in calls:
-                x = g.tensor.transpose(out, in_, T.ident[:])
-            return x
-        return node({"p": 0.02 + 128 * PEC * len(calls)}, deps, emit)
+    def dma(name, q, deps, out, in_, sem):
+        return step(name, q, deps, lambda: queues[q].dma_start(out, in_), sem, 16)
 
-    def dma(q, deps, out, in_, s, more=0.0, pri=0.0):
-        x = node({q: 0.05}, deps, lambda qq: queues[qq].dma_start(out, in_), s, 16, DMA + more)
-        x["pri"] = pri
-        return x
+    def iota(name, out, pattern, cm):
+        return step(name, "k", [], lambda: g.iota(out, pattern, 0, cm, allow_small_or_imprecise_dtypes=True))
 
-    def iota(out, n, pattern, base, cm):
-        return node({"k": 0.13 + 2 * n * CYC}, [], lambda q: g.iota(out, pattern, base, cm, allow_small_or_imprecise_dtypes=True))
-
-    d_gd = dma("s", [], T.gd[0], T.give[:], "gd")
-    d_give = dma("s", [], T.gi[:], T.give[:], "gs")
-    d_x = [dma("y", [], T.xi[:, 256 * h:256 * h + 256], T.x[:, 256 * h:256 * h + 256], "x%d" % h, 0.1 * h) for h in range(2)]
-    d_wire = dma("s", [], T.wi[:], T.wires[:], "wl")
-    tabs = [[], [], []]
-
-    def load_table(l, h, n, more, deps=()):
-        tabs[l].append(dma("y", list(deps), T.tab[16 * h:16 * h + 16 * n, l, :], T.tb[h:h + n, l * 65536:(l + 1) * 65536],
-                           "t%d%d" % (l, h // n % 4), more, -1000.0))
-
-    for h in (0, 2, 4):
-        load_table(0, h, 2, 1.5 + 0.4 * h)
-
-    s0 = 32 if r % 2 == 0 else -32
-    s1 = 64 if r < 2 else -64
-    k_pint = node({"k": 0.13}, [], lambda q: g.iota(T.pint[:, 0:1], [[0, 1]], 0, 1))
-    k_pf = iota(T.pf[:], 1, [[0, 1]], 0, 1)
-    k_jc = iota(T.jc[:], 128, [[1, 128]], 0, 0)
-    k_jl = iota(T.jl[:], 128, [[-s1, 2], [-s0, 2], [1, 32]], 32 * (r ^ 3), 0)
-    k_jr = iota(T.jr[:], 128, [[s1, 2], [s0, 2], [1, 32]], 32 * r, 0)
-    c_pz = V([], "set", T.pall[:], 0.0, cy=256)
-    c_ones = V([], "set", T.ones[:], 1.0)
-    c_lo = V([k_pint], "ts", T.pint[:, 2:3], T.pint[:, 0:1], 15, None, OP.bitwise_and)
-    c_low = V([c_lo], "copy", T.plow[:], T.pint[:, 2:3])
-    c_id = V([k_jc, k_pf], "ts", T.ident[:], T.jc[:], T.pf[:], None, OP.is_equal)
-    c_id4 = V([k_jc, k_pf], "ts", T.id4[:], T.jc[:], T.pf[:], None, OP.is_equal)
-    c_m16 = V([k_jc, c_low], "ts", T.m16[:], T.jc[:, 0:16], T.plow[:], None, OP.is_equal)
-    c_pall = []
-    for x2 in range(2):
-        for g2 in range(2):
-            c_pall.append(V([c_id4, c_pz], "copy", T.pall[:, x2, g2, :, x2, :], T.id4[:, :, g2, :]))
-
-    dst = {d: cores[r ^ d] for d in (1, 2, 3)}
+    dst = {d: T.cores[(r + d) % N] for d in (1, 2, 3)}
     far = [d for d in dst if topo.chip(dst[d]) != topo.chip(core)]
     near = [d for d in dst if d not in far]
     use = {}
@@ -218,183 +118,199 @@ def rank_program(g, core, T, topo):
         farset |= set(en)
         w = len(en) // len(far)
         use[d] = en[j * w:j * w + w]
-    for j, d in enumerate(near):
+    for d in near:
         en = [x for x in topo.engines(core, dst[d]) if x not in farset]
-        w = len(en) // len(near)
-        use[d] = en[j * w:j * w + w]
+        use[d] = en[::len(en) // NEAR]
     total_eng = sum(len(use[d]) for d in dst)
 
-    def send(deps, name, src, dest):
-        def emit(q):
+    def send(name, deps, sem, src, dest):
+        def emit():
             tr = []
             for d in (1, 2, 3):
                 rid, pid, _ = topo.addr(dst[d])
                 tr.append(RemoteDMATransfer(dst_ids=[DstId(rid=rid, pnc=pid)], dma_engine_mask=sum(1 << x for x in use[d]),
-                                            remote_sem=T.sem[name], src=src(d), dst=dest(d)))
+                                            remote_sem=T.sem[sem], src=src(d), dst=dest(d)))
             g.remote_dma_fused(tr, local_sem=T.sem.loc)
             return None
-        return node({"k": 0.6}, deps, emit, name, total_eng, REM - 0.6)
+        return step(name, "k", deps, emit, sem, total_eng)
 
-    arr, own = {}, {}
-    free = {"pr": None, "pl": None, "pw": None, "pv": None, "pa": None, "pm0": None, "pm1": None, "q1": None}
-    a_give = send([d_gd], "ga", lambda d: T.gd[0], lambda d: T.gd[d])
+    dma("gd", "s", [], T.gd[r], T.give[:], "gd")
+    dma("gi", "s", [], T.gi[:], T.give[:], "gs")
+    dma("wi", "s", [], T.wi[:], T.wires[:], "wl")
+    for c in range(2):
+        dma("x0%d" % c, "y", [], T.xi0[:, c, :], T.x[64 * c:64 * c + 64, 0:128], "x0")
+        dma("x1%d" % c, "y", [], T.xi1[:, c, :], T.x[64 * c:64 * c + 64, 128:512], "x1")
+    t0 = [dma("t0%d" % h, "y", ["zb0"] if h >= EARLY else [], T.tab[16 * h:16 * h + 32, 0, :], T.tb[h:h + 2, 0:65536], "t0")
+          for h in range(0, 8, 2)]
+    later = []
+    for h in range(8):
+        later.append(dma("t1%d" % h, "y", ["sb0" if h < TQ else later[-TQ]], T.tab[16 * h:16 * h + 16, 1, :], T.tb[h:h + 1, 65536:131072], "t1%d" % (h % 4)))
+    for h in range(16):
+        k, a, c = h // 4, h // 2 % 2, h % 2
+        later.append(dma("t2%d" % h, "y", [later[-TQ]], T.tab3[32 * k + 16 * a:32 * k + 16 * a + 16, 4096 * c:4096 * c + 4096],
+                         T.tb[2 * k + c:2 * k + c + 1, 131072:196608], "t2%d" % (h % 4)))
+    tabs = [t0, later[:8], later[8:]]
+    window = [T.tab[:, 0, :], T.tab[:, 1, :], T.tab3[:]]
 
-    xb, xt = [], []
-    for k in range(NBLK):
-        xb.append(V([d_x[k // 2]], "copy", T.xb[:, 128 * k:128 * k + 128], T.xi[:, 128 * k:128 * k + 128], cy=128))
-        xt.append(V([xb[k]], "tr", T.xt[:, k], T.xb[:, 128 * k:128 * k + 128]))
+    iota("jp", T.jp[:], [[16, 4], [64, 2], [1, 16]], 0)
+    iota("pf", T.pf[:], [[0, 1]], 1)
+    iota("jc", T.jc[:], [[1, 128]], 0)
+    iota("jm", T.jm[:], [[1, 16], [16, 8]], 0)
+    iota("wz0", T.wz[:, :, 0:9:2, :], [[0, 640]], 0)
+    V("ident", ["jc", "pf"], "ts", T.ident[:], T.jc[:], T.pf[:], None, OP.is_equal)
+    V("id4", ["jc", "pf"], "ts", T.id4[:], T.jc[:], T.pf[:], None, OP.is_equal)
+    V("big", [], "set", T.big[:], 4096.0)
+    V("mz0", [], "set", T.msk[:, 0:8, :], 0.0)
+    V("mz1", [], "set", T.msk[:, 8:16, :], 0.0)
+    V("msk", ["mz0", "mz1", "jm", "pf"], "ts", T.msk[:, :, 15:143:16], T.jm[:], T.pf[:], None, OP.is_equal)
 
-    c_gl = V([d_give], "copy", T.gl[:], T.gi[:])
-    c_dg = V([c_gl, k_jr, k_pf], "ts", T.dg[:], T.jr[:], T.pf[:], T.gl[:, 0:1], OP.is_equal, OP.mult)
-    a = MM([c_dg, c_ones], [(T.pw[:, 0:128], T.ones[:], T.dg[:], True, True, 128)])
-    free["pw"] = c_one = V([a, k_pf], "ts", T.one[:], T.pw[:, 0:128], T.pf[:], None, OP.is_equal, cy=128)
+    send("sg", ["gd"], "ga", lambda d: T.gd[r], lambda d: T.gd[r])
+    V("gl", ["gi"], "copy", T.gl[:], T.gi[:])
+    V("og0", ["gl", "jp"], "ts", T.og[:, 0, :], T.jp[:], T.gl[:, 0:1], None, OP.is_equal)
+    MM("po", ["og0", "ident"], [(T.pw[:, 0:128], T.og[:, 0, :], T.ident[:], True, True)])
+    S("one", ["po"], T.one[:], T.pw[:, 0:128])
+    for c in range(2):
+        V("xb0%d" % c, ["x00", "x01"], "copy", T.xb0[:, :, c, :], T.xi0[:, c, :])
+        V("xb1%d" % c, ["x10", "x11"], "copy", T.xb1[:, :, c, :], T.xi1[:, c, :])
+    V("xt0", ["xb00", "xb01"], "tr", T.xt0[:], T.xb0[:])
+    V("xt1", ["xb10", "xb11"], "tr", T.xt1[:], T.xb1[:])
+    turn = [(0, r, N - r)] + ([(N - r, 0, r)] if r else [])
+    MM("pl0", ["xt0", "one"], [(T.pl[:, 32 * s:32 * s + 32 * n], T.xt0[:], T.one[:, 32 * q:32 * q + 32 * n], True, True) for s, q, n in turn])
+    V("zb0", ["pl0"], "copy", T.zb0[:, 3:7, :], T.pl[:, 0:128])
+    send("sb0", ["zb0"], "b0", lambda d: T.zb0[:, 3 + d, :], lambda d: T.zb0[:, 3 - d, :])
+    MM("pl1", ["xt1", "one"], [(T.pv[:, s:s + n, i, :], T.xt1[:, 128 * i:128 * i + 128], T.one[:, 32 * q:32 * q + 32 * n], True, True)
+                               for i in range(3) for s, q, n in turn])
+    S("zb1", ["pl1"], T.zb1[:, 3:7], T.pv[:, :, 0:3, :])
+    send("sb1", ["zb1"], "b1", lambda d: T.zb1[:, 3 + d], lambda d: T.zb1[:, 3 - d])
 
-    def zslot(e, k):
-        for ci, blks in enumerate(SENDS[e]):
-            if k in blks:
-                return T["z%d_%d" % (e, ci)], "a%d_%d" % (e, ci), blks.index(k), blks
-
-    def post(e, k, deps, src, on):
-        z, name, i, blks = zslot(e, k)
-        if MODE[e] == "A":
-            own[(e, k)] = c = VS(deps, z[:, 3, i, :], src, 128, 128, on)
-        else:
-            c = VS(deps, T.cu[:, k, :], src, 128, 128, on)
-            a = MM([c, c_one, free["pl"]], [(T.pl[:, 0:128], T.cu[:, k, :], T.one[:], True, True, 128)])
-            free["pl"] = own[(e, k)] = VS([a], z[:, 3:7, i, :], T.pl[:, 0:128], 128, 128)
-        if k == blks[-1]:
-            n = send([own[(e, b)] for b in blks], name, lambda d: z[:, 3 if MODE[e] == "A" else 3 + d, :, :], lambda d: z[:, 3 - d, :, :])
-            for b in blks:
-                arr[(e, b)] = n
-        return c
-
-    for k in range(NBLK):
-        a = MM([xt[k], c_pall, free["q1"]], [(T.q1[:, 0:4, bp, :], T.pall[:, g2, bp], T.xt[:, k, :, g2, :], g2 == 0, g2 == 1, 64)
-                                             for bp in range(2) for g2 in range(2)])
-        free["q1"] = post(0, k, [a], T.q1[:, 0:4], "s" if k == 0 else "vs")
-    load_table(0, 6, 2, 2.5, [own[(0, 1)]])
-
-    X = {}
-    d_gg = [dma("y", [a_give if j < 3 else None], T.gg[32 * j:32 * j + 32, :],
-                T.gd[3 - j, 32 * r:32 * r + 32, :] if j < 3 else T.give[32 * r:32 * r + 32, :], "gg", 0.0, -500.0) for j in (3, 0, 1, 2)]
-    c_gb = X["gb"] = V([d_gg], "copy", T.gbs[:], T.gg[:])
-    c_wf = V([d_wire], "copy", T.wf[:], T.wi[:])
-    c_w = []
+    V("wf", ["wi"], "copy", T.wf[:], T.wi[:])
     for l in range(3):
-        o0 = V([c_wf, k_jl], "ts", T.oh[:, 2 * l, :], T.jl[:], T.wf[:, 2 * l:2 * l + 1], 64.0, OP.is_equal, OP.mult)
-        o1 = V([c_wf, k_jl], "ts", T.oh[:, 2 * l + 1, :], T.jl[:], T.wf[:, 2 * l + 1:2 * l + 2], None, OP.is_equal)
-        b = ["pm1", "pm0", "pa"][l]
-        a = MM([o0, o1, c_id, free[b]], [(T[b][:, 0:128], T.oh[:, 2 * l, :], T.ident[:], True, False, 128),
-                                         (T[b][:, 0:128], T.oh[:, 2 * l + 1, :], T.ident[:], False, True, 128)])
-        free[b] = c_wm = VS([a], T.wm[:, l, :], T[b][:, 0:128], 128, 128)
-        if MODE[l] == "B":
-            c_w.append([c_wm])
-            continue
-        c_og = X["og%d" % l] = V([c_gb, k_jc], "ts", T.og[:, l, :], T.jc[:], T.gbs[:, l:l + 1], None, OP.is_equal)
-        b = ["pw", "pv"][l % 2]
-        X["wm%d" % l] = []
-        a = free[b]
-        for j in range(4):
-            a = MM([c_wm, c_og, a], [(T[b][:, 128 * j:128 * j + 128], T.og[32 * j:32 * j + 32, l, :], T.wm[32 * j:32 * j + 32, l, :], True, True, 128)])
-            X["wm%d" % l].append(a)
-        free[b] = X["wc%d" % l] = VS([a], T.wc[:, l, :, :], T[b][:, 0:512], 512, 512, "s")
-        c_w.append([free[b]])
-    c_msk = [scaled([c_m16, c_id], T.msk[:, u, :], T.ident[:], T.m16[:, u:u + 1]) for u in range(16)]
+        V("oh%d" % (2 * l), ["wf", "jc"], "ts", T.oh[:, 2 * l, :], T.jc[:], T.wf[:, 2 * l:2 * l + 1], 64.0, OP.is_equal, OP.mult)
+        V("oh%d" % (2 * l + 1), ["wf", "jc"], "ts", T.oh[:, 2 * l + 1, :], T.jc[:], T.wf[:, 2 * l + 1:2 * l + 2], None, OP.is_equal)
+    MM("pwm0", ["oh0", "oh1", "ident"], [(T.pm1[32 * j:32 * j + 32, 0:128], T.oh[:, i, 32 * ((r + 1 + j) % N):32 * ((r + 1 + j) % N) + 32], T.ident[:], i == 0, i == 1)
+                                         for j in range(4) for i in range(2)])
+    S("wm0", ["pwm0"], T.wm[:, 0, :], T.pm1[:, 0:128])
+    MM("pwm1", ["oh2", "oh3", "ident"], [(T.pm0[:, 0:128], T.oh[:, 2 + i, :], T.ident[:], i == 0, i == 1) for i in range(2)])
+    S("wm1", ["pwm1"], T.wm[:, 1, :], T.pm0[:, 0:128])
+    MM("pwm2", ["oh4", "oh5", "id4", "zb0"], [(T.pl[:, 64 * c:64 * c + 64], T.oh[:, 4 + i, :], T.id4[:, :, c, :], i == 0, i == 1) for c in range(2) for i in range(2)])
+    S("wm2", ["pwm2"], T.wm[:, 2, :], T.pl[:, 0:128])
+    dma("gg", "y", ["sg", "gd"], T.gg[:], T.gd[:, 32 * r:32 * r + 32, :], "gg")
+    V("gb", ["gg"], "copy", T.gbs[:], T.gg[:])
+    for l in (1, 2):
+        V("og%d" % l, ["gb", "jc"], "ts", T.og[:, l, :], T.jc[:], T.gbs[:, l:l + 1], None, OP.is_equal)
+        a = "one" if l == 1 else "zb1"
+        for q in range(N):
+            out = T.pw[:, 128 * q:128 * q + 128] if l == 1 else T.pv[:, q]
+            a = MM("pw%d%d" % (l, q), ["wm%d" % l, "og%d" % l, a], [(out, T.og[32 * q:32 * q + 32, l, :], T.wm[32 * q:32 * q + 32, l, :], True, True)])
+    S("wc1", ["pw13"], T.wc[:], T.pw[:])
+    S("wc2", ["pw23", "wz0"], T.wz[:, :, 1:9:2, :], T.pv[:])
 
-    B = []
+    ranks = [(r + d) % N for d in range(N)]
+    order = {q: [] for q in queues}
+    MM("tr0", ["sb0", "zb0", "ident"], [(T.pr[:, 0, :], T.zb0[:, 0:4, :])])
+    V("lt0", ["tr0"], "copy", T.lt[:, 0], T.pr[:, 0, :])
+    MM("tr1", ["sb1", "zb1", "lt0"], [(T.pr[32 * j:32 * j + 32, 1, :], T.zb1[:, j, 0, :]) for j in range(4)])
+    V("lt1", ["tr1"], "copy", T.lt[:, 1], T.pr[:, 1, :])
+    MM("tr2", ["lt1"], [(T.pr[32 * j:32 * j + 32, 1 + i, :], T.zb1[:, j, i, :]) for i in (1, 2) for j in range(4)])
+    V("lt2", ["tr2"], "copy", T.lt[:, 2:4], T.pr[:, 2:4, :])
     for t in range(NT):
         l, k = divmod(t, NBLK)
-        pm = "pm%d" % (t % 2)
-        o = {}
-        B.append(o)
-        for q in EXTRA.get(t, {}):
-            o["x" + q] = []
-            for n in EXTRA[t][q]:
-                o["x" + q] += X[n] if isinstance(X[n], list) else [X[n]]
-        z, _, i, blks = zslot(l, k)
-        if MODE[l] == "A":
-            o["a"] = MM([arr[(l, k)], own[(l, k)], c_w[l], free["pa"]],
-                        [(T.pa[:, 0:128], T.wc[:, l, j, :], z[:, j, i, :], j == 3, j == 2, 128) for j in (3, 0, 1, 2)])
+        pa, pm = T["pa%d" % (t % 2)], T["pm%d" % (t % 2)]
+        free = "off%d" % (t - 2) if t >= 2 else None
+        if l == 0:
+            MM("a%d" % t, ["lt%d" % min(t, 2), "wm0", free], [(pa[:, 2 * a:2 * a + 2], T.wm[:, 0, :], T.lt[:, t, :, a], True, True) for a in range(2)])
+        elif l == 1:
+            MM("a%d" % t, ["sz%d" % (t - 4), "pms%d" % (t - 4), "wc1", free],
+               [(pa[:, 0:4], T.wc[:, q, :], T.z[:, t - 4, q], q == ranks[0], q == ranks[-1]) for q in ranks])
         else:
-            o["tr"] = TR([arr[(l, k)], own[(l, k)], free["pr"], c_id],
-                         [(T.pr[:, 0, :], z[:, 0:4, 0, :])] if len(blks) == 1 else [(T.pr[32 * j:32 * j + 32, 0, :], z[:, j, i, :]) for j in range(4)])
-            o["lt"] = free["pr"] = VS([o["tr"]], T.lt[:, t, :], T.pr[:, 0, :], 64, 128, "v")
-            o["a"] = MM([o["lt"], c_w[l], free["pa"]], [(T.pa[:, 0:128], T.wm[:, l, :], T.lt[:, t, :], True, True, 128)])
-        o["off"] = free["pa"] = V([o["a"]], "copy", T.off[:, t, :], T.pa[:, 0:128], cy=128)
-        if t == 0:
-            for l2 in (1, 2):
-                for h in range(8):
-                    load_table(l2, h, 1, 0.6, [arr[(0, 0)] if l2 == 1 and h < TQ[1] else (tabs[1] + tabs[2])[-TQ[l2]]])
+            calls = []
+            for c in range(2):
+                if c:
+                    calls.append((pa[:, 0:4, c, :], T.ident[:], T.big[:], True, False))
+                calls += [(pa[:, 0:4, c, :], T.wz[:, 2 * q + c, 1 - a:9 - a, :], T.z[:, t - 4, q, :, a, :], not c and not a and q == ranks[0], a == 1 and q == ranks[-1])
+                          for q in ranks for a in range(2)]
+            MM("a%d" % t, ["sz%d" % (t - 4), "pms%d" % (t - 4), "wc2", "big", free], calls)
+        V("off%d" % t, ["a%d" % t], "copy", T.off[:, t, :], pa[:, 0:4])
 
-        def gather(q, b, n):
-            x = VS([o["off"], tabs[l]], T.gt[:, t, 16 * b:16 * b + 16 * n], T.tab[:, l, :].indirect(T.off[:, t, b:b + n]),
-                   16 * n * GAT / CYC, 16 * n * GAT / CYC, q)
-            j = 1 if "g%s0" % q in o else 0
-            o["g%s%d" % (q, j)] = x
-            return x
+        def gather(name, q, b, n):
+            out, win = T.gt[:, t, 16 * b:16 * b + 16 * n], window[l].indirect(T.off[:, t, b:b + n])
+            deps = ["off%d" % t] + tabs[l]
+            return V(name, deps, "copy", out, win) if q == "v" else S(name, deps, out, win)
 
-        ms = []
-        for h, (lo, w, calls) in enumerate(pieces(t)):
-            gs = [gather(q, b, n) for q, b, n in calls]
-            o["m%d" % h] = MM([gs, free[pm], c_msk],
-                              [(T[pm][:, lo:lo + w], T.msk[:, u, :], T.gt[:, t, 16 * lo + u:16 * lo + 16 * w:16], u == 0, u == 15, max(64, w))
-                               for u in range(16)])
-            ms.append(o["m%d" % h])
+        def merge(name, deps, bank, lo, w):
+            return MM(name, deps + ["msk"], [(bank[:, lo:lo + w], T.msk[:, u, 15 - u:143 - u], T.gt[:, t, 16 * lo + u:16 * lo + 16 * w:16], u == 0, u == 15)
+                                             for u in range(16)])
+
+        def store(name, dep, h, n):
+            c0 = 16 * (BASE[k] + h * SPAN[k])
+            return dma(name, "y", [dep], T.y[:, c0:c0 + 64 * n], T.yo[:, k, 64 * h:64 * h + 64 * n], "yd")
+
+        held = ["wm1", "wm0"][t] if t < 2 else ("pms%d" if t < 10 else "z%d") % (t - 2)
+        if t == NT - 1:
+            gs = [gather("g%d_%d" % (t, j), q, b, n) for j, (q, b, n) in enumerate(LAST)]
+            merge("m0_%d" % t, gs[0:2] + [held], pm, 0, 64)
+            merge("m1_%d" % t, gs[2:4] + ["wm2"], T.pl, 64, 64)
+            V("z11a", ["m0_%d" % t], "tr", T.yo[:, k, 0:64], pm[:, 0:64])
+            V("z11b", ["m1_%d" % t], "tr", T.yo[:, k, 64:128], T.pl[:, 64:128])
+            order["v"] += [gs[0], "z10", gs[2], "z11a", "z11b"]
+            order["s"] += [gs[1], gs[3]]
+            order["p"] += ["m1_10", "m0_11", "m1_11"]
+            order["y"] += [store("y11a", "z11a", 0, 1), store("y11b", "z11b", 1, 1)]
+            continue
+        gs, b = [], 0
+        for x in VSEQ[t]:
+            if isinstance(x, int):
+                gs.append((gather("g%d_%d" % (t, len(gs)), "v", b, x), b + x))
+                b += x
+            order["v"].append(gs[-1][0] if isinstance(x, int) else x)
+        order["s"] += SX.get(t, []) + [gather("gs%d" % t, "s", b, 128 - b)]
+        cut = gs[-2][1] if isinstance(VSEQ[t][-1], int) else b
+        if l == 2:
+            cut = 0
+        else:
+            merge("m0_%d" % t, [x[0] for x in gs if x[1] <= cut] + [held], pm, 0, cut)
+        merge("m1_%d" % t, [x[0] for x in gs] + ["gs%d" % t, held], pm, cut, 128 - cut)
         if l < 2:
-            o["pms"] = free[pm] = post(l + 1, k, ms, T[pm][:, 0:128], "v")
+            V("pms%d" % t, ["m0_%d" % t, "m1_%d" % t], "copy", T.z[:, t, r], pm[:, 0:128])
+            order["k"].append(send("sz%d" % t, ["pms%d" % t], "a%d" % t, lambda d, t=t: T.z[:, t, r], lambda d, t=t: T.z[:, t, r]))
         else:
-            o["pms"] = free[pm] = VS(ms, T.pms[:, k], T[pm][:, 0:128], 128, 128, "v")
-            o["otr"] = MM([o["pms"], free["q1"], c_pall], [(T.q1[:, 0:4, g2, :], T.pall[:, x2, g2], T.pms[:, k, :, x2, :], x2 == 0, x2 == 1, 64)
-                                                           for g2 in range(2) for x2 in range(2)])
-            o["z"] = free["q1"] = V([o["otr"]], "tr", T.yo[:, 128 * k:128 * k + 128], T.q1[:, 0:4], cy=128)
-            dma("y", [o["z"]], T.y[:, 128 * k:128 * k + 128], T.yo[:, 128 * k:128 * k + 128], "yd")
-    last = {}
+            V("z%d" % t, ["m1_%d" % t], "tr", T.yo[:, k, :], pm[:, 0:128])
+            order["y"] += [store("y%d" % t, "z%d" % t, 0, 2)] if SPAN[k] == 4 else [store("y%d%s" % (t, "ab"[h]), "z%d" % t, h, 1) for h in range(2)]
+        both = ["m1_%d" % (t - 1), "a%d" % (t + 1)]
+        order["p"] += ["tr1", "a1", "tr2"] if t == 0 else both if t <= 8 else both[::-1]
+        order["p"] += [x + str(q) for x in PX.get(t, []) for q in range(N)] + ([] if l == 2 else ["m0_%d" % t])
 
-    def then(q, *names):
-        for t, name in names:
-            if 0 <= t < NT and name in B[t]:
-                x = B[t][name]
-                for n in (x if isinstance(x, list) else [x]):
-                    if q in n["dur"]:
-                        n["prev"] = last.get(q)
-                        last[q] = n
+    order["k"][:0] = ["jp", "pf", "jc", "sg", "sb0", "jm", "sb1", "wz0"]
+    order["v"][:0] = ["mz0", "ident", "gl", "xb00", "og0", "xb01", "wf", "xt0", "oh0", "oh1", "zb0", "xb10", "xb11", "oh2", "xt1", "oh3",
+                      "oh4", "oh5", "id4", "big", "mz1", "msk", "lt0", "off0"]
+    order["s"][:0] = ["gd", "gi", "wi", "one", "wm0", "zb1", "wm1", "wm2"]
+    order["p"][:0] = ["po", "pl0", "pwm0", "pl1", "pwm1", "pwm2", "tr0", "a0"]
+    order["y"][:0] = ["x00", "x01", "x10", "x11"] + t0 + ["gg"] + later
 
-    way = [c_gl, xb[0], c_dg, xt[0], c_one, xb[1]]
-    for n, p in zip(way[1:], way):
-        n["prev"] = p
-    for n in c_msk:
-        n["prev"] = own[(0, 0)]
-    then("v", (0, "lt"), (0, "off"))
-    then("p", (0, "tr"), (0, "a"))
-    for t in range(NT + 1):
-        steps(then, t)
-
-    order = layout(nodes)
     total = {}
-    for n in order:
-        s = n["sem"] or n["q"]
-        total[s] = total.get(s, 0) + n["n"]
-        n["tok"] = (s, total[s])
-    waited = {}
-
-    def wait(q, s, val):
-        if waited.get((q, s), 0) < val:
-            queues[q].wait_ge(T.sem[s], val)
-            waited[(q, s)] = val
-
+    for q in order:
+        for name in order[q]:
+            n = steps[name]
+            total[n["sem"]] = n["tok"] = total.get(n["sem"], 0) + n["n"]
+    assert sum(len(o) for o in order.values()) == len(steps)
     sent = 0
-    for n in order:
-        need = {}
-        for d in n["deps"]:
-            s, val = d["tok"]
-            need[s] = max(need.get(s, 0), val)
-        for s in sorted(need):
-            wait(n["q"], s, need[s])
-        x = n["emit"](n["q"])
-        if x is None:
-            sent += n["n"]
-        else:
-            x.then_inc(T.sem[n["tok"][0]], n["n"])
+    for q in order:
+        waited = {}
+        for name in order[q]:
+            n = steps[name]
+            need = {}
+            for d in n["deps"]:
+                s = steps[d]["sem"]
+                need[s] = max(need.get(s, 0), steps[d]["tok"])
+            for s in sorted(need):
+                if waited.get(s, 0) < need[s]:
+                    queues[q].wait_ge(T.sem[s], need[s])
+                    waited[s] = need[s]
+            x = n["emit"]()
+            if x is None:
+                sent += n["n"]
+            else:
+                x.then_inc(T.sem[n["sem"]], n["n"])
     for s in sorted(total):
-        wait("y", s, total[s])
-    wait("y", "loc", sent)
+        g.sync.wait_ge(T.sem[s], total[s])
+    g.sync.wait_ge(T.sem.loc, sent)

@@ -6,30 +6,41 @@ COPY = ActivationFunctionType.Copy
 N = 4
 NBLK = 4
 NT = 3 * NBLK
-BASE, SPAN = [0, 8, 12, 16], [4, 12, 12, 12]
-EARLY = 6
-TQ = 4
+LOADS = [[0, 1], [2, 3]]
+SENDS = [([0, 1], "v"), ([2, 3], "s")]
+TURNS = [[0, 1], [2, 3]]
+EARLY = 8
+LATE = "xb10"
+TQ = 8
 NEAR = 8
+START = {
+    "k": ["jp", "pf", "jc", "sg", "sb0", "jm", "sb1", "big", "wz0"],
+    "v": ["mz0", "ident", "gl", "og0", "xb00", "xb01", "wf", "xt0", "oh0", "oh1", "zb0", "xb10", "xb11", "oh2", "xt1", "oh3",
+          "oh4", "oh5", "msk", "lt0", "off0", "off1"],
+    "s": ["gi", "gd", "wi", "mz1", "one", "id4", "wm0", "zb1", "wm1", "wm2"],
+    "p": ["po", "pl0", "pwm0", "pl1", "pwm1", "pwm2", "tr0", "a0", "a1"],
+}
 VSEQ = [
-    [44, "lt1", 10, "off1", 6],
-    [40, "pms0", "lt2", "gb", "off2", 8],
-    [44, "pms1", "og1", "off3", 8, "og2"],
-    [44, "pms2", 12, "off4", 6],
-    [44, "pms3", 8, "off5", 6],
-    [44, "pms4", 8, "off6", 6],
-    [44, "pms5", 12, "off7", 6],
-    [44, "pms6", 8, "off8", 6],
-    [44, "pms7", 8, "off9", 6],
-    [30, "off10", 28, "z8"],
-    [30, "off11", 28, "z9"],
+    [58, "lt1", "gb"],
+    [52, "off2", "pms0", "og1"],
+    [62, "pms1", "og2"],
+    [72, "off4", "pms2"],
+    [60, "off5", "pms3"],
+    [62, "off6", "pms4"],
+    [72, "off7", "pms5"],
+    [60, "off8", "pms6"],
+    [62, "off9", "pms7"],
+    [60, "off10", "z8"],
+    [60, "off11", "z9"],
 ]
 SX = {3: ["wc1"], 6: ["wc2"]}
-PX = {2: ["pw1"], 4: ["pw2"]}
+PSEQ = {0: ["tr1"], 1: ["a2", "m0", "n0m"], 2: ["m1", "n1m", "pw1"], 3: ["m2", "o4", "e4", "a4", "n2m", "o5"],
+        4: ["m3", "e5", "a5", "n3m", "o6", "pw2"], 6: ["m5", "e7", "a7", "n5m"], 7: ["m6", "o8", "e8", "a8", "n6m", "o9"]}
+CUT = [13, 12, 9]
 LAST = [("v", 0, 36), ("s", 36, 28), ("v", 64, 22), ("s", 86, 42)]
 
 SCRATCH = {
-    "xi0": ("sbuf", [128, 2, 64], "int32"),
-    "xi1": ("sbuf", [128, 2, 192], "int32"),
+    "xi": ("sbuf", [128, 2, 256], "int32"),
     "gi": ("sbuf", [128, 3], "int32"),
     "gd": ("dram", [4, 128, 3], "int32"),
     "gg": ("sbuf", [128, 3], "int32"),
@@ -42,7 +53,7 @@ SCRATCH = {
     "pf": ("sbuf", [128, 1], "float32"),
     "ident": ("sbuf", [128, 128], "bfloat16"),
     "id4": ("sbuf", [128, 4, 2, 16], "bfloat16"),
-    "big": ("sbuf", [128, 64], "bfloat16"),
+    "big": ("sbuf", [128, 4, 2, 16], "bfloat16"),
     "msk": ("sbuf", [128, 16, 144], "bfloat16"),
     "gl": ("sbuf", [128, 3], "float32"),
     "gbs": ("sbuf", [128, 3], "float32"),
@@ -53,12 +64,8 @@ SCRATCH = {
     "wm": ("sbuf", [128, 3, 128], "bfloat16"),
     "wc": ("sbuf", [128, 4, 128], "bfloat16"),
     "wz": ("sbuf", [128, 8, 9, 16], "bfloat16"),
-    "xb0": ("sbuf", [128, 4, 2, 16], "bfloat16"),
-    "xb1": ("sbuf", [128, 12, 2, 16], "bfloat16"),
-    "xt0": ("sbuf", [128, 128], "bfloat16"),
-    "xt1": ("sbuf", [128, 384], "bfloat16"),
-    "zb0": ("sbuf", [128, 7, 32], "bfloat16"),
-    "zb1": ("sbuf", [128, 7, 3, 32], "bfloat16"),
+    "xb": ("sbuf", [128, 16, 2, 16], "bfloat16"),
+    "xt": ("sbuf", [128, 512], "bfloat16"),
     "lt": ("sbuf", [128, NBLK, 64, 2], "bfloat16"),
     "z": ("sbuf", [128, 8, 4, 4, 2, 16], "bfloat16"),
     "off": ("sbuf", [128, NT, 128], "uint16"),
@@ -68,13 +75,15 @@ SCRATCH = {
     "pm1": ("psum", [128, 512], "float32"),
     "pa0": ("psum", [128, 16, 2, 16], "float32"),
     "pa1": ("psum", [128, 16, 2, 16], "float32"),
-    "pw": ("psum", [128, 512], "float32"),
-    "pl": ("psum", [128, 512], "float32"),
-    "pv": ("psum", [128, 4, 4, 32], "float32"),
+    "pw": ("psum", [128, 4, 4, 32], "float32"),
+    "pl": ("psum", [128, 256, 2], "float32"),
+    "pv": ("psum", [128, 256, 2], "float32"),
     "pr": ("psum", [128, 8, 128], "bfloat16"),
 }
-SEMAPHORES = ["v", "p", "s", "k", "x0", "x1", "gs", "gd", "gg", "ga", "wl", "yd", "loc", "b0", "b1", "t0"]
-SEMAPHORES += ["t%d%d" % (_l, _q) for _l in (1, 2) for _q in range(4)] + ["a%d" % _t for _t in range(8)]
+for _i in range(2):
+    SCRATCH["zb%d" % _i] = ("sbuf", [128, 7, 32, 2], "bfloat16")
+SEMAPHORES = ["v", "p", "s", "k", "gs", "gd", "gg", "ga", "wl", "yd", "loc", "t0", "x0", "x1", "x2", "b0", "b1", "b2"]
+SEMAPHORES += ["t%d%d" % (_l, _q) for _l in (1, 2) for _q in range(8)] + [_s + str(_t) for _t in range(8) for _s in "an"]
 
 
 def rank_program(g, core, T, topo):
@@ -94,6 +103,9 @@ def rank_program(g, core, T, topo):
 
     def S(name, deps, out, in_):
         return step(name, "s", deps, lambda: g.scalar.activation(out, in_, COPY))
+
+    def copy(name, q, deps, out, in_):
+        return V(name, deps, "copy", out, in_) if q == "v" else S(name, deps, out, in_)
 
     def MM(name, deps, calls):
         def emit():
@@ -122,33 +134,39 @@ def rank_program(g, core, T, topo):
         en = [x for x in topo.engines(core, dst[d]) if x not in farset]
         use[d] = en[::len(en) // NEAR]
     total_eng = sum(len(use[d]) for d in dst)
+    landed = {}
 
-    def send(name, deps, sem, src, dest):
+    def send(name, deps, sem, src, dest, early=None):
         def emit():
             tr = []
-            for d in (1, 2, 3):
+            for d in far + near:
                 rid, pid, _ = topo.addr(dst[d])
                 tr.append(RemoteDMATransfer(dst_ids=[DstId(rid=rid, pnc=pid)], dma_engine_mask=sum(1 << x for x in use[d]),
-                                            remote_sem=T.sem[sem], src=src(d), dst=dest(d)))
+                                            remote_sem=T.sem[early if early and d in near else sem], src=src(d), dst=dest(d)))
             g.remote_dma_fused(tr, local_sem=T.sem.loc)
             return None
-        return step(name, "k", deps, emit, sem, total_eng)
+        if early:
+            landed[early] = {"sem": early, "tok": NEAR}
+        return step(name, "k", deps, emit, sem, total_eng - (NEAR if early else 0))
 
     dma("gd", "s", [], T.gd[r], T.give[:], "gd")
     dma("gi", "s", [], T.gi[:], T.give[:], "gs")
     dma("wi", "s", [], T.wi[:], T.wires[:], "wl")
-    for c in range(2):
-        dma("x0%d" % c, "y", [], T.xi0[:, c, :], T.x[64 * c:64 * c + 64, 0:128], "x0")
-        dma("x1%d" % c, "y", [], T.xi1[:, c, :], T.x[64 * c:64 * c + 64, 128:512], "x1")
-    t0 = [dma("t0%d" % h, "y", ["zb0"] if h >= EARLY else [], T.tab[16 * h:16 * h + 32, 0, :], T.tb[h:h + 2, 0:65536], "t0")
+    xs, base, span = [], {}, {}
+    for i, bl in enumerate(LOADS):
+        lo, hi = bl[0], bl[-1] + 1
+        xs += [dma("x%d%d" % (i, c), "y", [], T.xi[:, c, 64 * lo:64 * hi], T.x[64 * c:64 * c + 64, 128 * lo:128 * hi], "x%d" % i) for c in range(2)]
+        for k in bl:
+            base[k], span[k] = 4 * (lo + k), 4 * len(bl)
+    t0 = [dma("t0%d" % h, "y", [LATE] if h >= EARLY else [], T.tab[16 * h:16 * h + 32, 0, :], T.tb[h:h + 2, 0:65536], "t0")
           for h in range(0, 8, 2)]
     later = []
     for h in range(8):
-        later.append(dma("t1%d" % h, "y", ["sb0" if h < TQ else later[-TQ]], T.tab[16 * h:16 * h + 16, 1, :], T.tb[h:h + 1, 65536:131072], "t1%d" % (h % 4)))
+        later.append(dma("t1%d" % h, "y", ["sb0" if h < TQ else later[-TQ]], T.tab[16 * h:16 * h + 16, 1, :], T.tb[h:h + 1, 65536:131072], "t1%d" % (h % TQ)))
     for h in range(16):
         k, a, c = h // 4, h // 2 % 2, h % 2
         later.append(dma("t2%d" % h, "y", [later[-TQ]], T.tab3[32 * k + 16 * a:32 * k + 16 * a + 16, 4096 * c:4096 * c + 4096],
-                         T.tb[2 * k + c:2 * k + c + 1, 131072:196608], "t2%d" % (h % 4)))
+                         T.tb[2 * k + c:2 * k + c + 1, 131072:196608], "t2%d" % (h % TQ)))
     tabs = [t0, later[:8], later[8:]]
     window = [T.tab[:, 0, :], T.tab[:, 1, :], T.tab3[:]]
 
@@ -157,31 +175,44 @@ def rank_program(g, core, T, topo):
     iota("jc", T.jc[:], [[1, 128]], 0)
     iota("jm", T.jm[:], [[1, 16], [16, 8]], 0)
     iota("wz0", T.wz[:, :, 0:9:2, :], [[0, 640]], 0)
+    iota("big", T.big[:], [[0, 4], [4096, 2], [0, 16]], 0)
     V("ident", ["jc", "pf"], "ts", T.ident[:], T.jc[:], T.pf[:], None, OP.is_equal)
-    V("id4", ["jc", "pf"], "ts", T.id4[:], T.jc[:], T.pf[:], None, OP.is_equal)
-    V("big", [], "set", T.big[:], 4096.0)
-    V("mz0", [], "set", T.msk[:, 0:8, :], 0.0)
-    V("mz1", [], "set", T.msk[:, 8:16, :], 0.0)
+    S("id4", ["ident"], T.id4[:], T.ident[:])
+    V("mz0", [], "set", T.msk[:, 0:10, :], 0.0)
+    S("mz1", ["mz0"], T.msk[:, 10:16, :], T.msk[:, 0:6, :])
     V("msk", ["mz0", "mz1", "jm", "pf"], "ts", T.msk[:, :, 15:143:16], T.jm[:], T.pf[:], None, OP.is_equal)
 
     send("sg", ["gd"], "ga", lambda d: T.gd[r], lambda d: T.gd[r])
     V("gl", ["gi"], "copy", T.gl[:], T.gi[:])
     V("og0", ["gl", "jp"], "ts", T.og[:, 0, :], T.jp[:], T.gl[:, 0:1], None, OP.is_equal)
-    MM("po", ["og0", "ident"], [(T.pw[:, 0:128], T.og[:, 0, :], T.ident[:], True, True)])
-    S("one", ["po"], T.one[:], T.pw[:, 0:128])
-    for c in range(2):
-        V("xb0%d" % c, ["x00", "x01"], "copy", T.xb0[:, :, c, :], T.xi0[:, c, :])
-        V("xb1%d" % c, ["x10", "x11"], "copy", T.xb1[:, :, c, :], T.xi1[:, c, :])
-    V("xt0", ["xb00", "xb01"], "tr", T.xt0[:], T.xb0[:])
-    V("xt1", ["xb10", "xb11"], "tr", T.xt1[:], T.xb1[:])
+    MM("po", ["og0", "ident"], [(T.pw[:, 0], T.og[:, 0, :], T.ident[:], True, True)])
+    S("one", ["po"], T.one[:], T.pw[:, 0])
+    for i, bl in enumerate(LOADS):
+        lo, hi = bl[0], bl[-1] + 1
+        for c in range(2):
+            V("xb%d%d" % (i, c), ["x%d0" % i, "x%d1" % i], "copy", T.xb[:, 4 * lo:4 * hi, c, :], T.xi[:, c, 64 * lo:64 * hi])
+        V("xt%d" % i, ["xb%d0" % i, "xb%d1" % i], "tr", T.xt[:, 128 * lo:128 * hi], T.xb[:, 4 * lo:4 * hi])
     turn = [(0, r, N - r)] + ([(N - r, 0, r)] if r else [])
-    MM("pl0", ["xt0", "one"], [(T.pl[:, 32 * s:32 * s + 32 * n], T.xt0[:], T.one[:, 32 * q:32 * q + 32 * n], True, True) for s, q, n in turn])
-    V("zb0", ["pl0"], "copy", T.zb0[:, 3:7, :], T.pl[:, 0:128])
-    send("sb0", ["zb0"], "b0", lambda d: T.zb0[:, 3 + d, :], lambda d: T.zb0[:, 3 - d, :])
-    MM("pl1", ["xt1", "one"], [(T.pv[:, s:s + n, i, :], T.xt1[:, 128 * i:128 * i + 128], T.one[:, 32 * q:32 * q + 32 * n], True, True)
-                               for i in range(3) for s, q, n in turn])
-    S("zb1", ["pl1"], T.zb1[:, 3:7], T.pv[:, :, 0:3, :])
-    send("sb1", ["zb1"], "b1", lambda d: T.zb1[:, 3 + d], lambda d: T.zb1[:, 3 - d])
+    lines = {}
+    for i, (bl, q) in enumerate(SENDS):
+        bank, zb = [T.pl, T.pv][i], T["zb%d" % i]
+        xt = "xt%d" % [bl[0] in b for b in LOADS].index(True)
+        MM("pl%d" % i, [xt, "one"], [(bank[:, 32 * s:32 * s + 32 * w, j], T.xt[:, 128 * k:128 * k + 128], T.one[:, 32 * o:32 * o + 32 * w], True, True)
+                                     for j, k in enumerate(bl) for s, o, w in turn])
+        copy("zb%d" % i, q, ["pl%d" % i], zb[:, 3:7], bank[:, 0:128])
+        send("sb%d" % i, ["zb%d" % i], "b%d" % i, lambda d, zb=zb: zb[:, 3 + d], lambda d, zb=zb: zb[:, 3 - d])
+        for j, k in enumerate(bl):
+            lines[k] = (i, zb, j)
+    turned = {}
+    for n, blocks in enumerate(TURNS):
+        calls, deps = [], ["ident", "lt%d" % (n - 1) if n else None]
+        for k in blocks:
+            i, zb, j = lines[k]
+            calls.append((T.pr[:, k, :], zb[:, 0:4, :, j]))
+            deps += ["sb%d" % i, "zb%d" % i]
+            turned[k] = "lt%d" % n
+        MM("tr%d" % n, deps, calls)
+        V("lt%d" % n, ["tr%d" % n], "copy", T.lt[:, blocks[0]:blocks[-1] + 1], T.pr[:, blocks[0]:blocks[-1] + 1, :])
 
     V("wf", ["wi"], "copy", T.wf[:], T.wi[:])
     for l in range(3):
@@ -192,100 +223,88 @@ def rank_program(g, core, T, topo):
     S("wm0", ["pwm0"], T.wm[:, 0, :], T.pm1[:, 0:128])
     MM("pwm1", ["oh2", "oh3", "ident"], [(T.pm0[:, 0:128], T.oh[:, 2 + i, :], T.ident[:], i == 0, i == 1) for i in range(2)])
     S("wm1", ["pwm1"], T.wm[:, 1, :], T.pm0[:, 0:128])
-    MM("pwm2", ["oh4", "oh5", "id4", "zb0"], [(T.pl[:, 64 * c:64 * c + 64], T.oh[:, 4 + i, :], T.id4[:, :, c, :], i == 0, i == 1) for c in range(2) for i in range(2)])
-    S("wm2", ["pwm2"], T.wm[:, 2, :], T.pl[:, 0:128])
+    MM("pwm2", ["oh4", "oh5", "id4", "zb0"], [(T.pl[:, 32 * c:32 * c + 32], T.oh[:, 4 + i, :], T.id4[:, :, c, :], i == 0, i == 1) for c in range(2) for i in range(2)])
+    S("wm2", ["pwm2"], T.wm[:, 2, :], T.pl[:, 0:64])
     dma("gg", "y", ["sg", "gd"], T.gg[:], T.gd[:, 32 * r:32 * r + 32, :], "gg")
     V("gb", ["gg"], "copy", T.gbs[:], T.gg[:])
+    chains = {}
     for l in (1, 2):
         V("og%d" % l, ["gb", "jc"], "ts", T.og[:, l, :], T.jc[:], T.gbs[:, l:l + 1], None, OP.is_equal)
         a = "one" if l == 1 else "zb1"
+        chains["pw%d" % l] = []
         for q in range(N):
-            out = T.pw[:, 128 * q:128 * q + 128] if l == 1 else T.pv[:, q]
+            out = T.pw[:, q] if l == 1 else T.pv[:, 64 * q:64 * q + 64]
             a = MM("pw%d%d" % (l, q), ["wm%d" % l, "og%d" % l, a], [(out, T.og[32 * q:32 * q + 32, l, :], T.wm[32 * q:32 * q + 32, l, :], True, True)])
+            chains["pw%d" % l].append(a)
     S("wc1", ["pw13"], T.wc[:], T.pw[:])
     S("wc2", ["pw23", "wz0"], T.wz[:, :, 1:9:2, :], T.pv[:])
 
-    ranks = [(r + d) % N for d in range(N)]
-    order = {q: [] for q in queues}
-    MM("tr0", ["sb0", "zb0", "ident"], [(T.pr[:, 0, :], T.zb0[:, 0:4, :])])
-    V("lt0", ["tr0"], "copy", T.lt[:, 0], T.pr[:, 0, :])
-    MM("tr1", ["sb1", "zb1", "lt0"], [(T.pr[32 * j:32 * j + 32, 1, :], T.zb1[:, j, 0, :]) for j in range(4)])
-    V("lt1", ["tr1"], "copy", T.lt[:, 1], T.pr[:, 1, :])
-    MM("tr2", ["lt1"], [(T.pr[32 * j:32 * j + 32, 1 + i, :], T.zb1[:, j, i, :]) for i in (1, 2) for j in range(4)])
-    V("lt2", ["tr2"], "copy", T.lt[:, 2:4], T.pr[:, 2:4, :])
+    ranks = [(r + d) % N for d in [0] + near + far]
+    order = {q: list(START.get(q, [])) for q in queues}
+    order["y"] = xs + t0 + ["gg"] + later
     for t in range(NT):
         l, k = divmod(t, NBLK)
         pa, pm = T["pa%d" % (t % 2)], T["pm%d" % (t % 2)]
-        free = "off%d" % (t - 2) if t >= 2 else None
+        free = {0: None, 1: None, 5: "off1"}.get(t, "off%d" % (t - 2))
         if l == 0:
-            MM("a%d" % t, ["lt%d" % min(t, 2), "wm0", free], [(pa[:, 2 * a:2 * a + 2], T.wm[:, 0, :], T.lt[:, t, :, a], True, True) for a in range(2)])
-        elif l == 1:
-            MM("a%d" % t, ["sz%d" % (t - 4), "pms%d" % (t - 4), "wc1", free],
-               [(pa[:, 0:4], T.wc[:, q, :], T.z[:, t - 4, q], q == ranks[0], q == ranks[-1]) for q in ranks])
+            n = 2 if t == 2 else 1
+            if t < 3:
+                MM("a%d" % t, [turned[t], turned[t + n - 1], "wm0", free],
+                   [(pa[:, 4 * i + 2 * a:4 * i + 2 * a + 2], T.wm[:, 0, :], T.lt[:, t + i, :, a], True, True) for i in range(n) for a in range(2)])
+                V("off%d" % t, ["a%d" % t], "copy", T.off[:, t:t + n, :], pa[:, 0:4 * n])
         else:
-            calls = []
-            for c in range(2):
-                if c:
-                    calls.append((pa[:, 0:4, c, :], T.ident[:], T.big[:], True, False))
-                calls += [(pa[:, 0:4, c, :], T.wz[:, 2 * q + c, 1 - a:9 - a, :], T.z[:, t - 4, q, :, a, :], not c and not a and q == ranks[0], a == 1 and q == ranks[-1])
-                          for q in ranks for a in range(2)]
-            MM("a%d" % t, ["sz%d" % (t - 4), "pms%d" % (t - 4), "wc2", "big", free], calls)
-        V("off%d" % t, ["a%d" % t], "copy", T.off[:, t, :], pa[:, 0:4])
+            if l == 1:
+                calls = [(pa[:, 0:4], T.wc[:, q, :], T.z[:, t - 4, q], q == ranks[0], q == ranks[-1]) for q in ranks]
+            else:
+                calls = [(pa[:, 0:4], T.ident[:], T.big[:], True, False)]
+                calls += [(pa[:, 0:4, c, :], T.wz[:, 2 * q + c, 1 - a:9 - a, :], T.z[:, t - 4, q, :, a, :], False, q == ranks[-1] and a == 1 and c == 1)
+                          for q in ranks for c in range(2) for a in range(2)]
+            w = len(calls) // N
+            MM("o%d" % t, ["pms%d" % (t - 4), "wc%d" % l, "big", free], calls[:-3 * w])
+            MM("e%d" % t, ["n%d" % (t - 4)], calls[-3 * w:-len(far) * w])
+            MM("a%d" % t, ["sz%d" % (t - 4)], calls[-len(far) * w:])
+            V("off%d" % t, ["a%d" % t], "copy", T.off[:, t, :], pa[:, 0:4])
 
         def gather(name, q, b, n):
-            out, win = T.gt[:, t, 16 * b:16 * b + 16 * n], window[l].indirect(T.off[:, t, b:b + n])
-            deps = ["off%d" % t] + tabs[l]
-            return V(name, deps, "copy", out, win) if q == "v" else S(name, deps, out, win)
+            return copy(name, q, ["off%d" % (2 if t == 3 else t)] + tabs[l], T.gt[:, t, 16 * b:16 * b + 16 * n], window[l].indirect(T.off[:, t, b:b + n]))
 
-        def merge(name, deps, bank, lo, w):
-            return MM(name, deps + ["msk"], [(bank[:, lo:lo + w], T.msk[:, u, 15 - u:143 - u], T.gt[:, t, 16 * lo + u:16 * lo + 16 * w:16], u == 0, u == 15)
-                                             for u in range(16)])
+        def merge(name, deps, out, lo, w, units=range(16)):
+            return MM(name, deps + ["msk"], [(out, T.msk[:, u, 15 - u:143 - u], T.gt[:, t, 16 * lo + u:16 * lo + 16 * w:16], u == 0, u == 15)
+                                             for u in units])
 
         def store(name, dep, h, n):
-            c0 = 16 * (BASE[k] + h * SPAN[k])
+            c0 = 16 * (base[k] + h * span[k])
             return dma(name, "y", [dep], T.y[:, c0:c0 + 64 * n], T.yo[:, k, 64 * h:64 * h + 64 * n], "yd")
 
         held = ["wm1", "wm0"][t] if t < 2 else ("pms%d" if t < 10 else "z%d") % (t - 2)
         if t == NT - 1:
             gs = [gather("g%d_%d" % (t, j), q, b, n) for j, (q, b, n) in enumerate(LAST)]
-            merge("m0_%d" % t, gs[0:2] + [held], pm, 0, 64)
-            merge("m1_%d" % t, gs[2:4] + ["wm2"], T.pl, 64, 64)
-            V("z11a", ["m0_%d" % t], "tr", T.yo[:, k, 0:64], pm[:, 0:64])
-            V("z11b", ["m1_%d" % t], "tr", T.yo[:, k, 64:128], T.pl[:, 64:128])
+            merge("m11a", gs[0:2] + [held], pm[:, 0:64], 0, 64)
+            merge("m11b", gs[2:4] + ["wm2"], T.pl[:, 0:32], 64, 64)
+            V("z11a", ["m11a"], "tr", T.yo[:, k, 0:64], pm[:, 0:64])
+            V("z11b", ["m11b"], "tr", T.yo[:, k, 64:128], T.pl[:, 0:32])
             order["v"] += [gs[0], "z10", gs[2], "z11a", "z11b"]
             order["s"] += [gs[1], gs[3]]
-            order["p"] += ["m1_10", "m0_11", "m1_11"]
+            order["p"] += ["m10", "n10m", "m11a", "m11b"]
             order["y"] += [store("y11a", "z11a", 0, 1), store("y11b", "z11b", 1, 1)]
             continue
         gs, b = [], 0
         for x in VSEQ[t]:
             if isinstance(x, int):
-                gs.append((gather("g%d_%d" % (t, len(gs)), "v", b, x), b + x))
+                gs.append(gather("g%d_%d" % (t, len(gs)), "v", b, x))
                 b += x
-            order["v"].append(gs[-1][0] if isinstance(x, int) else x)
+            order["v"].append(gs[-1] if isinstance(x, int) else x)
         order["s"] += SX.get(t, []) + [gather("gs%d" % t, "s", b, 128 - b)]
-        cut = gs[-2][1] if isinstance(VSEQ[t][-1], int) else b
-        if l == 2:
-            cut = 0
-        else:
-            merge("m0_%d" % t, [x[0] for x in gs if x[1] <= cut] + [held], pm, 0, cut)
-        merge("m1_%d" % t, [x[0] for x in gs] + ["gs%d" % t, held], pm, cut, 128 - cut)
+        merge("m%d" % t, gs + ["gs%d" % t, held], pm[:, 0:128], 0, 128, range(CUT[l]))
+        merge("n%dm" % t, [], pm[:, 0:128], 0, 128, range(CUT[l], 16))
         if l < 2:
-            V("pms%d" % t, ["m0_%d" % t, "m1_%d" % t], "copy", T.z[:, t, r], pm[:, 0:128])
-            order["k"].append(send("sz%d" % t, ["pms%d" % t], "a%d" % t, lambda d, t=t: T.z[:, t, r], lambda d, t=t: T.z[:, t, r]))
+            V("pms%d" % t, ["n%dm" % t], "copy", T.z[:, t, r], pm[:, 0:128])
+            order["k"].append(send("sz%d" % t, ["pms%d" % t], "a%d" % t, lambda d, t=t: T.z[:, t, r], lambda d, t=t: T.z[:, t, r], "n%d" % t))
         else:
-            V("z%d" % t, ["m1_%d" % t], "tr", T.yo[:, k, :], pm[:, 0:128])
-            order["y"] += [store("y%d" % t, "z%d" % t, 0, 2)] if SPAN[k] == 4 else [store("y%d%s" % (t, "ab"[h]), "z%d" % t, h, 1) for h in range(2)]
-        both = ["m1_%d" % (t - 1), "a%d" % (t + 1)]
-        order["p"] += ["tr1", "a1", "tr2"] if t == 0 else both if t <= 8 else both[::-1]
-        order["p"] += [x + str(q) for x in PX.get(t, []) for q in range(N)] + ([] if l == 2 else ["m0_%d" % t])
-
-    order["k"][:0] = ["jp", "pf", "jc", "sg", "sb0", "jm", "sb1", "wz0"]
-    order["v"][:0] = ["mz0", "ident", "gl", "xb00", "og0", "xb01", "wf", "xt0", "oh0", "oh1", "zb0", "xb10", "xb11", "oh2", "xt1", "oh3",
-                      "oh4", "oh5", "id4", "big", "mz1", "msk", "lt0", "off0"]
-    order["s"][:0] = ["gd", "gi", "wi", "one", "wm0", "zb1", "wm1", "wm2"]
-    order["p"][:0] = ["po", "pl0", "pwm0", "pl1", "pwm1", "pwm2", "tr0", "a0"]
-    order["y"][:0] = ["x00", "x01", "x10", "x11"] + t0 + ["gg"] + later
+            V("z%d" % t, ["n%dm" % t], "tr", T.yo[:, k, :], pm[:, 0:128])
+            order["y"] += [store("y%d" % t, "z%d" % t, 0, 2)] if span[k] == 4 else [store("y%d%s" % (t, "ab"[h]), "z%d" % t, h, 1) for h in range(2)]
+        for x in PSEQ.get(t, ["m%d" % (t - 1), "e%d" % (t + 1), "a%d" % (t + 1), "n%dm" % (t - 1), "o%d" % (t + 2)]):
+            order["p"] += chains.get(x, [x] if x != "o%d" % NT else [])
 
     total = {}
     for q in order:
@@ -293,7 +312,9 @@ def rank_program(g, core, T, topo):
             n = steps[name]
             total[n["sem"]] = n["tok"] = total.get(n["sem"], 0) + n["n"]
     assert sum(len(o) for o in order.values()) == len(steps)
+    steps.update(landed)
     sent = 0
+    seen = {}
     for q in order:
         waited = {}
         for name in order[q]:
@@ -306,11 +327,13 @@ def rank_program(g, core, T, topo):
                 if waited.get(s, 0) < need[s]:
                     queues[q].wait_ge(T.sem[s], need[s])
                     waited[s] = need[s]
+                    seen[s] = max(seen.get(s, 0), need[s])
             x = n["emit"]()
             if x is None:
-                sent += n["n"]
+                sent += total_eng
             else:
                 x.then_inc(T.sem[n["sem"]], n["n"])
+    g.wait_ge(T.sem.loc, sent)
     for s in sorted(total):
-        g.sync.wait_ge(T.sem[s], total[s])
-    g.sync.wait_ge(T.sem.loc, sent)
+        if seen.get(s, 0) < total[s]:
+            g.sync.wait_ge(T.sem[s], total[s])

@@ -6,38 +6,45 @@ COPY = ActivationFunctionType.Copy
 N = 4
 NBLK = 4
 NT = 3 * NBLK
-LOADS = [[0, 1], [2, 3]]
-SENDS = [([0, 1], "v"), ([2, 3], "s")]
-TURNS = [[0, 1], [2, 3]]
-EARLY = 8
-LATE = "xb10"
+GROUPS = [([0], "v"), ([1], "s"), ([2, 3], "s")]
 TQ = 8
 NEAR = 8
 START = {
-    "k": ["jp", "pf", "jc", "sg", "sb0", "jm", "sb1", "big", "wz0"],
-    "v": ["mz0", "ident", "gl", "og0", "xb00", "xb01", "wf", "xt0", "oh0", "oh1", "zb0", "xb10", "xb11", "oh2", "xt1", "oh3",
-          "oh4", "oh5", "msk", "lt0", "off0", "off1"],
-    "s": ["gi", "gd", "wi", "mz1", "one", "id4", "wm0", "zb1", "wm1", "wm2"],
-    "p": ["po", "pl0", "pwm0", "pl1", "pwm1", "pwm2", "tr0", "a0", "a1"],
+    "k": ["jp", "pf", "jc", "sg", "sb0", "sb1", "jm", "sb2", "big", "wz0"],
+    "v": ["col0", "mz0", "ident", "og0", "xb00", "xb01", "wf", "xt0", "xb10", "xb11", "oh0", "oh1", "xt1", "zb0", "xb20", "xb21", "oh2", "oh3", "xt2",
+          "oh4", "oh5", "col1", "col2", "msk", "off0"],
+    "s": ["gi", "gd", "wi", "mz1", "one", "id4", "zb1", "wm0", "zb2", "wm1", "wm2"],
+    "p": ["po", "pl0", "pl1", "pwm0", "pl2", "pwm1", "pwm2", "o0", "e0", "a0"],
 }
 VSEQ = [
-    [58, "lt1", "gb"],
-    [52, "off2", "pms0", "og1"],
-    [62, "pms1", "og2"],
-    [72, "off4", "pms2"],
-    [60, "off5", "pms3"],
-    [62, "off6", "pms4"],
-    [72, "off7", "pms5"],
-    [60, "off8", "pms6"],
-    [62, "off9", "pms7"],
-    [60, "off10", "z8"],
-    [60, "off11", "z9"],
+    [54, "off1", "og1"],
+    [52, "off2", "og2", "pms0"],
+    [68, "pms1"],
+    [66, "pms2", "off4"],
+    [54, "pms3", "off5"],
+    [54, "pms4", "off6"],
+    [54, "pms5", "off7"],
+    [56, "pms6", "off8"],
+    [56, "pms7", "off9"],
+    [62, "off10", "z8"],
+    [58, "off11", "z9"],
 ]
-SX = {3: ["wc1"], 6: ["wc2"]}
-PSEQ = {0: ["tr1"], 1: ["a2", "m0", "n0m"], 2: ["m1", "n1m", "pw1"], 3: ["m2", "o4", "e4", "a4", "n2m", "o5"],
-        4: ["m3", "e5", "a5", "n3m", "o6", "pw2"], 6: ["m5", "e7", "a7", "n5m"], 7: ["m6", "o8", "e8", "a8", "n6m", "o9"]}
-CUT = [13, 12, 9]
-LAST = [("v", 0, 36), ("s", 36, 28), ("v", 64, 22), ("s", 86, 42)]
+SSEQ = [[74], [76], ["wc1", 60], ["wc2", 62], [74], [74], [74], [72], [72], [66], [70]]
+PSEQ = [
+    ["o1", "e1", "a1", "o2", "e2"],
+    ["a2", "pw10", 5, "pw11", 5, "pw12", 6, "pw13"],
+    ["pw20", 5, "pw21", 5, "pw22", 6, "pw23", "o4", "h2_1"],
+    [16, "e4", "a4", "o5", "h3_1"],
+    [16, "e5", "a5", "o6", "h4_1"],
+    [16, "e6", "a6", "o7", "h5_1"],
+    [16, "e7", "a7", "o8", "h6_1"],
+    [16, "e8", "a8", "o9", "h7_1"],
+    [16, "e9", "a9", "o10"],
+    [9, "e10", "a10", 7, "o11"],
+    [10, "e11", "a11", 6],
+    [16, "m11a", "m11b"],
+]
+LAST = [("v", 0, 32), ("s", 32, 32), ("v", 64, 30), ("s", 94, 34)]
 
 SCRATCH = {
     "xi": ("sbuf", [128, 2, 256], "int32"),
@@ -51,22 +58,21 @@ SCRATCH = {
     "jp": ("sbuf", [128, 128], "bfloat16"),
     "jm": ("sbuf", [128, 128], "bfloat16"),
     "pf": ("sbuf", [128, 1], "float32"),
+    "col": ("sbuf", [128, 3, 8], "uint16"),
     "ident": ("sbuf", [128, 128], "bfloat16"),
     "id4": ("sbuf", [128, 4, 2, 16], "bfloat16"),
     "big": ("sbuf", [128, 4, 2, 16], "bfloat16"),
     "msk": ("sbuf", [128, 16, 144], "bfloat16"),
-    "gl": ("sbuf", [128, 3], "float32"),
-    "gbs": ("sbuf", [128, 3], "float32"),
     "og": ("sbuf", [128, 3, 128], "bfloat16"),
     "one": ("sbuf", [128, 128], "bfloat16"),
     "wf": ("sbuf", [128, 6], "float32"),
     "oh": ("sbuf", [128, 6, 128], "bfloat16"),
+    "wr": ("sbuf", [128, 4, 128], "bfloat16"),
     "wm": ("sbuf", [128, 3, 128], "bfloat16"),
     "wc": ("sbuf", [128, 4, 128], "bfloat16"),
     "wz": ("sbuf", [128, 8, 9, 16], "bfloat16"),
     "xb": ("sbuf", [128, 16, 2, 16], "bfloat16"),
-    "xt": ("sbuf", [128, 512], "bfloat16"),
-    "lt": ("sbuf", [128, NBLK, 64, 2], "bfloat16"),
+    "xt": ("sbuf", [128, NBLK, 64, 2], "bfloat16"),
     "z": ("sbuf", [128, 8, 4, 4, 2, 16], "bfloat16"),
     "off": ("sbuf", [128, NT, 128], "uint16"),
     "gt": ("sbuf", [128, NT, 2048], "bfloat16"),
@@ -75,14 +81,13 @@ SCRATCH = {
     "pm1": ("psum", [128, 512], "float32"),
     "pa0": ("psum", [128, 16, 2, 16], "float32"),
     "pa1": ("psum", [128, 16, 2, 16], "float32"),
-    "pw": ("psum", [128, 4, 4, 32], "float32"),
-    "pl": ("psum", [128, 256, 2], "float32"),
-    "pv": ("psum", [128, 256, 2], "float32"),
-    "pr": ("psum", [128, 8, 128], "bfloat16"),
+    "pw": ("psum", [128, 512], "float32"),
+    "pl": ("psum", [128, 512], "float32"),
+    "pv": ("psum", [128, 512], "float32"),
 }
-for _i in range(2):
-    SCRATCH["zb%d" % _i] = ("sbuf", [128, 7, 32, 2], "bfloat16")
-SEMAPHORES = ["v", "p", "s", "k", "gs", "gd", "gg", "ga", "wl", "yd", "loc", "t0", "x0", "x1", "x2", "b0", "b1", "b2"]
+for _i in range(3):
+    SCRATCH["zb%d" % _i] = ("sbuf", [128, 4, 128 * len(GROUPS[_i][0])], "bfloat16")
+SEMAPHORES = ["v", "p", "s", "k", "gs", "gd", "gg", "ga", "wl", "yd", "loc", "t0"] + [_s + str(_i) for _i in range(3) for _s in "xbc"]
 SEMAPHORES += ["t%d%d" % (_l, _q) for _l in (1, 2) for _q in range(8)] + [_s + str(_t) for _t in range(8) for _s in "an"]
 
 
@@ -98,7 +103,8 @@ def rank_program(g, core, T, topo):
         return name
 
     def V(name, deps, call, *a):
-        f = {"copy": g.vector.tensor_copy, "ts": g.vector.tensor_scalar, "tr": g.vector.transpose, "set": g.vector.memset}[call]
+        f = {"copy": g.vector.tensor_copy, "ts": g.vector.tensor_scalar, "tt": g.vector.tensor_tensor, "tr": g.vector.transpose,
+             "set": g.vector.memset}[call]
         return step(name, "v", deps, lambda: f(*a))
 
     def S(name, deps, out, in_):
@@ -110,7 +116,7 @@ def rank_program(g, core, T, topo):
     def MM(name, deps, calls):
         def emit():
             for c in calls:
-                x = g.tensor.matmul(*c) if len(c) == 5 else g.tensor.transpose(c[0], c[1], T.ident[:])
+                x = g.tensor.matmul(*c)
             return x
         return step(name, "p", deps, emit)
 
@@ -136,13 +142,13 @@ def rank_program(g, core, T, topo):
     total_eng = sum(len(use[d]) for d in dst)
     landed = {}
 
-    def send(name, deps, sem, src, dest, early=None):
+    def send(name, deps, sem, part, early=None):
         def emit():
             tr = []
             for d in far + near:
                 rid, pid, _ = topo.addr(dst[d])
                 tr.append(RemoteDMATransfer(dst_ids=[DstId(rid=rid, pnc=pid)], dma_engine_mask=sum(1 << x for x in use[d]),
-                                            remote_sem=T.sem[early if early and d in near else sem], src=src(d), dst=dest(d)))
+                                            remote_sem=T.sem[early if early and d in near else sem], src=part, dst=part))
             g.remote_dma_fused(tr, local_sem=T.sem.loc)
             return None
         if early:
@@ -153,13 +159,12 @@ def rank_program(g, core, T, topo):
     dma("gi", "s", [], T.gi[:], T.give[:], "gs")
     dma("wi", "s", [], T.wi[:], T.wires[:], "wl")
     xs, base, span = [], {}, {}
-    for i, bl in enumerate(LOADS):
+    for i, (bl, _) in enumerate(GROUPS):
         lo, hi = bl[0], bl[-1] + 1
         xs += [dma("x%d%d" % (i, c), "y", [], T.xi[:, c, 64 * lo:64 * hi], T.x[64 * c:64 * c + 64, 128 * lo:128 * hi], "x%d" % i) for c in range(2)]
         for k in bl:
             base[k], span[k] = 4 * (lo + k), 4 * len(bl)
-    t0 = [dma("t0%d" % h, "y", [LATE] if h >= EARLY else [], T.tab[16 * h:16 * h + 32, 0, :], T.tb[h:h + 2, 0:65536], "t0")
-          for h in range(0, 8, 2)]
+    t0 = [dma("t0%d" % h, "y", [], T.tab[16 * h:16 * h + 32, 0, :], T.tb[h:h + 2, 0:65536], "t0") for h in range(0, 8, 2)]
     later = []
     for h in range(8):
         later.append(dma("t1%d" % h, "y", ["sb0" if h < TQ else later[-TQ]], T.tab[16 * h:16 * h + 16, 1, :], T.tb[h:h + 1, 65536:131072], "t1%d" % (h % TQ)))
@@ -176,66 +181,48 @@ def rank_program(g, core, T, topo):
     iota("jm", T.jm[:], [[1, 16], [16, 8]], 0)
     iota("wz0", T.wz[:, :, 0:9:2, :], [[0, 640]], 0)
     iota("big", T.big[:], [[0, 4], [4096, 2], [0, 16]], 0)
+    for l in range(3):
+        V("col%d" % l, [], "set", T.col[:, l, :], l)
     V("ident", ["jc", "pf"], "ts", T.ident[:], T.jc[:], T.pf[:], None, OP.is_equal)
     S("id4", ["ident"], T.id4[:], T.ident[:])
     V("mz0", [], "set", T.msk[:, 0:10, :], 0.0)
     S("mz1", ["mz0"], T.msk[:, 10:16, :], T.msk[:, 0:6, :])
     V("msk", ["mz0", "mz1", "jm", "pf"], "ts", T.msk[:, :, 15:143:16], T.jm[:], T.pf[:], None, OP.is_equal)
 
-    send("sg", ["gd"], "ga", lambda d: T.gd[r], lambda d: T.gd[r])
-    V("gl", ["gi"], "copy", T.gl[:], T.gi[:])
-    V("og0", ["gl", "jp"], "ts", T.og[:, 0, :], T.jp[:], T.gl[:, 0:1], None, OP.is_equal)
-    MM("po", ["og0", "ident"], [(T.pw[:, 0], T.og[:, 0, :], T.ident[:], True, True)])
-    S("one", ["po"], T.one[:], T.pw[:, 0])
-    for i, bl in enumerate(LOADS):
+    send("sg", ["gd"], "ga", T.gd[r])
+    V("og0", ["gi", "jp", "col0"], "tt", T.og[:, 0, :], T.gi[:].indirect(T.col[:, 0, :]), T.jp[:], OP.is_equal)
+    MM("po", ["og0", "ident"], [(T.pw[:, 0:128], T.og[:, 0, :], T.ident[:], True, True)])
+    S("one", ["po"], T.one[:], T.pw[:, 0:128])
+    for i, (bl, q) in enumerate(GROUPS):
         lo, hi = bl[0], bl[-1] + 1
+        bank, zb = [T.pl, T.pv, T.pw][i], T["zb%d" % i]
         for c in range(2):
             V("xb%d%d" % (i, c), ["x%d0" % i, "x%d1" % i], "copy", T.xb[:, 4 * lo:4 * hi, c, :], T.xi[:, c, 64 * lo:64 * hi])
-        V("xt%d" % i, ["xb%d0" % i, "xb%d1" % i], "tr", T.xt[:, 128 * lo:128 * hi], T.xb[:, 4 * lo:4 * hi])
-    turn = [(0, r, N - r)] + ([(N - r, 0, r)] if r else [])
-    lines = {}
-    for i, (bl, q) in enumerate(SENDS):
-        bank, zb = [T.pl, T.pv][i], T["zb%d" % i]
-        xt = "xt%d" % [bl[0] in b for b in LOADS].index(True)
-        MM("pl%d" % i, [xt, "one"], [(bank[:, 32 * s:32 * s + 32 * w, j], T.xt[:, 128 * k:128 * k + 128], T.one[:, 32 * o:32 * o + 32 * w], True, True)
-                                     for j, k in enumerate(bl) for s, o, w in turn])
-        copy("zb%d" % i, q, ["pl%d" % i], zb[:, 3:7], bank[:, 0:128])
-        send("sb%d" % i, ["zb%d" % i], "b%d" % i, lambda d, zb=zb: zb[:, 3 + d], lambda d, zb=zb: zb[:, 3 - d])
-        for j, k in enumerate(bl):
-            lines[k] = (i, zb, j)
-    turned = {}
-    for n, blocks in enumerate(TURNS):
-        calls, deps = [], ["ident", "lt%d" % (n - 1) if n else None]
-        for k in blocks:
-            i, zb, j = lines[k]
-            calls.append((T.pr[:, k, :], zb[:, 0:4, :, j]))
-            deps += ["sb%d" % i, "zb%d" % i]
-            turned[k] = "lt%d" % n
-        MM("tr%d" % n, deps, calls)
-        V("lt%d" % n, ["tr%d" % n], "copy", T.lt[:, blocks[0]:blocks[-1] + 1], T.pr[:, blocks[0]:blocks[-1] + 1, :])
+        V("xt%d" % i, ["xb%d0" % i, "xb%d1" % i], "tr", T.xt[:, lo:hi], T.xb[:, 4 * lo:4 * hi])
+        MM("pl%d" % i, ["xt%d" % i, "one"], [(bank[:, 128 * j + 64 * a:128 * j + 64 * a + 64], T.one[:], T.xt[:, k, :, a], True, True)
+                                             for j, k in enumerate(bl) for a in range(2)])
+        copy("zb%d" % i, q, ["pl%d" % i], zb[:, r, :], bank[:, 0:128 * len(bl)])
+        send("sb%d" % i, ["zb%d" % i], "b%d" % i, zb[:, r, :], "c%d" % i)
 
     V("wf", ["wi"], "copy", T.wf[:], T.wi[:])
     for l in range(3):
         V("oh%d" % (2 * l), ["wf", "jc"], "ts", T.oh[:, 2 * l, :], T.jc[:], T.wf[:, 2 * l:2 * l + 1], 64.0, OP.is_equal, OP.mult)
         V("oh%d" % (2 * l + 1), ["wf", "jc"], "ts", T.oh[:, 2 * l + 1, :], T.jc[:], T.wf[:, 2 * l + 1:2 * l + 2], None, OP.is_equal)
-    MM("pwm0", ["oh0", "oh1", "ident"], [(T.pm1[32 * j:32 * j + 32, 0:128], T.oh[:, i, 32 * ((r + 1 + j) % N):32 * ((r + 1 + j) % N) + 32], T.ident[:], i == 0, i == 1)
-                                         for j in range(4) for i in range(2)])
-    S("wm0", ["pwm0"], T.wm[:, 0, :], T.pm1[:, 0:128])
+    mine = slice(32 * r, 32 * r + 32)
+    MM("pwm0", ["oh0", "oh1", "ident"], [(T.pm1[mine, 128 * q:128 * q + 128], T.oh[:, i, 32 * q:32 * q + 32], T.ident[:], i == 0, i == 1)
+                                         for q in range(N) for i in range(2)])
+    S("wm0", ["pwm0"], T.wr[mine], T.pm1[mine, :])
     MM("pwm1", ["oh2", "oh3", "ident"], [(T.pm0[:, 0:128], T.oh[:, 2 + i, :], T.ident[:], i == 0, i == 1) for i in range(2)])
     S("wm1", ["pwm1"], T.wm[:, 1, :], T.pm0[:, 0:128])
-    MM("pwm2", ["oh4", "oh5", "id4", "zb0"], [(T.pl[:, 32 * c:32 * c + 32], T.oh[:, 4 + i, :], T.id4[:, :, c, :], i == 0, i == 1) for c in range(2) for i in range(2)])
-    S("wm2", ["pwm2"], T.wm[:, 2, :], T.pl[:, 0:64])
+    MM("pwm2", ["oh4", "oh5", "id4", "zb0"], [(T.pl[:, 64 * c:64 * c + 64], T.oh[:, 4 + i, :], T.id4[:, :, c, :], i == 0, i == 1) for c in range(2) for i in range(2)])
+    S("wm2", ["pwm2"], T.wm[:, 2, :], T.pl[:, 0:128])
     dma("gg", "y", ["sg", "gd"], T.gg[:], T.gd[:, 32 * r:32 * r + 32, :], "gg")
-    V("gb", ["gg"], "copy", T.gbs[:], T.gg[:])
-    chains = {}
     for l in (1, 2):
-        V("og%d" % l, ["gb", "jc"], "ts", T.og[:, l, :], T.jc[:], T.gbs[:, l:l + 1], None, OP.is_equal)
-        a = "one" if l == 1 else "zb1"
-        chains["pw%d" % l] = []
+        V("og%d" % l, ["gg", "jc", "col%d" % l], "tt", T.og[:, l, :], T.gg[:].indirect(T.col[:, l, :]), T.jc[:], OP.is_equal)
+        a = "zb2" if l == 1 else "zb1"
         for q in range(N):
-            out = T.pw[:, q] if l == 1 else T.pv[:, 64 * q:64 * q + 64]
+            out = (T.pw if l == 1 else T.pv)[:, 128 * q:128 * q + 128]
             a = MM("pw%d%d" % (l, q), ["wm%d" % l, "og%d" % l, a], [(out, T.og[32 * q:32 * q + 32, l, :], T.wm[32 * q:32 * q + 32, l, :], True, True)])
-            chains["pw%d" % l].append(a)
     S("wc1", ["pw13"], T.wc[:], T.pw[:])
     S("wc2", ["pw23", "wz0"], T.wz[:, :, 1:9:2, :], T.pv[:])
 
@@ -244,26 +231,30 @@ def rank_program(g, core, T, topo):
     order["y"] = xs + t0 + ["gg"] + later
     for t in range(NT):
         l, k = divmod(t, NBLK)
+        u = 0
+        for x in PSEQ[t]:
+            order["p"].append("m%d_%d" % (t - 1, u) if isinstance(x, int) else x)
+            u += x if isinstance(x, int) else 0
         pa, pm = T["pa%d" % (t % 2)], T["pm%d" % (t % 2)]
-        free = {0: None, 1: None, 5: "off1"}.get(t, "off%d" % (t - 2))
+        n = 2 if t == 2 else 1
         if l == 0:
-            n = 2 if t == 2 else 1
-            if t < 3:
-                MM("a%d" % t, [turned[t], turned[t + n - 1], "wm0", free],
-                   [(pa[:, 4 * i + 2 * a:4 * i + 2 * a + 2], T.wm[:, 0, :], T.lt[:, t + i, :, a], True, True) for i in range(n) for a in range(2)])
-                V("off%d" % t, ["a%d" % t], "copy", T.off[:, t:t + n, :], pa[:, 0:4 * n])
+            calls = [(pa[:, 0:4 * n], T.wr[mine, q, :], T["zb%d" % min(t, 2)][mine, q, :], q == ranks[0], q == ranks[-1]) for q in ranks]
+            need = [["zb%d" % t, "wm0"], "c%d" % t, "sb%d" % t]
+        elif l == 1:
+            calls = [(pa[:, 0:4], T.wc[:, q, :], T.z[:, t - 4, q], q == ranks[0], q == ranks[-1]) for q in ranks]
         else:
-            if l == 1:
-                calls = [(pa[:, 0:4], T.wc[:, q, :], T.z[:, t - 4, q], q == ranks[0], q == ranks[-1]) for q in ranks]
-            else:
-                calls = [(pa[:, 0:4], T.ident[:], T.big[:], True, False)]
-                calls += [(pa[:, 0:4, c, :], T.wz[:, 2 * q + c, 1 - a:9 - a, :], T.z[:, t - 4, q, :, a, :], False, q == ranks[-1] and a == 1 and c == 1)
-                          for q in ranks for c in range(2) for a in range(2)]
+            calls = [(pa[:, 0:4], T.ident[:], T.big[:], True, False)]
+            calls += [(pa[:, 0:4, c, :], T.wz[:, 2 * q + c, 1 - a:9 - a, :], T.z[:, t - 4, q, :, a, :], False, q == ranks[-1] and a == 1 and c == 1)
+                      for q in ranks for c in range(2) for a in range(2)]
+        if l:
+            need = [["pms%d" % (t - 4), "wc%d" % l, "big"], "n%d" % (t - 4), "sz%d" % (t - 4)]
+        if t != 3:
             w = len(calls) // N
-            MM("o%d" % t, ["pms%d" % (t - 4), "wc%d" % l, "big", free], calls[:-3 * w])
-            MM("e%d" % t, ["n%d" % (t - 4)], calls[-3 * w:-len(far) * w])
-            MM("a%d" % t, ["sz%d" % (t - 4)], calls[-len(far) * w:])
-            V("off%d" % t, ["a%d" % t], "copy", T.off[:, t, :], pa[:, 0:4])
+            free = {0: None, 1: None, 5: "off1"}.get(t, "off%d" % (t - 2))
+            MM("o%d" % t, need[0] + [free], calls[:-3 * w])
+            MM("e%d" % t, [need[1]], calls[-3 * w:-len(far) * w])
+            MM("a%d" % t, [need[2]], calls[-len(far) * w:])
+            V("off%d" % t, ["a%d" % t], "copy", T.off[:, t:t + n, :], pa[:, 0:4 * n])
 
         def gather(name, q, b, n):
             return copy(name, q, ["off%d" % (2 if t == 3 else t)] + tabs[l], T.gt[:, t, 16 * b:16 * b + 16 * n], window[l].indirect(T.off[:, t, b:b + n]))
@@ -280,31 +271,40 @@ def rank_program(g, core, T, topo):
         if t == NT - 1:
             gs = [gather("g%d_%d" % (t, j), q, b, n) for j, (q, b, n) in enumerate(LAST)]
             merge("m11a", gs[0:2] + [held], pm[:, 0:64], 0, 64)
-            merge("m11b", gs[2:4] + ["wm2"], T.pl[:, 0:32], 64, 64)
+            merge("m11b", gs[2:4] + ["wm2"], T.pl[:, 0:64], 64, 64)
             V("z11a", ["m11a"], "tr", T.yo[:, k, 0:64], pm[:, 0:64])
-            V("z11b", ["m11b"], "tr", T.yo[:, k, 64:128], T.pl[:, 0:32])
-            order["v"] += [gs[0], "z10", gs[2], "z11a", "z11b"]
+            V("z11b", ["m11b"], "tr", T.yo[:, k, 64:128], T.pl[:, 0:64])
+            order["v"] += [gs[0], gs[2], "z10", "z11a", "z11b"]
             order["s"] += [gs[1], gs[3]]
-            order["p"] += ["m10", "n10m", "m11a", "m11b"]
             order["y"] += [store("y11a", "z11a", 0, 1), store("y11b", "z11b", 1, 1)]
             continue
+        seq = {"v": VSEQ[t], "s": SSEQ[t]}
+        calls = sorted((j, q != "v", q, n) for q in seq for j, n in enumerate([x for x in seq[q] if isinstance(x, int)]))
         gs, b = [], 0
-        for x in VSEQ[t]:
-            if isinstance(x, int):
-                gs.append(gather("g%d_%d" % (t, len(gs)), "v", b, x))
-                b += x
-            order["v"].append(gs[-1] if isinstance(x, int) else x)
-        order["s"] += SX.get(t, []) + [gather("gs%d" % t, "s", b, 128 - b)]
-        merge("m%d" % t, gs + ["gs%d" % t, held], pm[:, 0:128], 0, 128, range(CUT[l]))
-        merge("n%dm" % t, [], pm[:, 0:128], 0, 128, range(CUT[l], 16))
+        for j, _, q, n in calls:
+            gs.append(gather("g%d_%s%d" % (t, q, j), q, b, n))
+            b += n
+        assert b == 128
+        for q in seq:
+            j = 0
+            for x in seq[q]:
+                order[q].append("g%d_%s%d" % (t, q, j) if isinstance(x, int) else x)
+                j += isinstance(x, int)
+        lo, u = 0, 0
+        for n in (1, 2):
+            if "h%d_%d" % (t, n) in PSEQ[t] + PSEQ[t + 1]:
+                lo = sum(c[3] for c in calls[:n])
+                merge("h%d_%d" % (t, n), gs[:n] + [held], pm[:, 0:lo], 0, lo)
+        for n in PSEQ[t + 1]:
+            if isinstance(n, int):
+                last = merge("m%d_%d" % (t, u), gs + [held], pm[:, lo:128], lo, 128 - lo, range(u, u + n))
+                u += n
         if l < 2:
-            V("pms%d" % t, ["n%dm" % t], "copy", T.z[:, t, r], pm[:, 0:128])
-            order["k"].append(send("sz%d" % t, ["pms%d" % t], "a%d" % t, lambda d, t=t: T.z[:, t, r], lambda d, t=t: T.z[:, t, r], "n%d" % t))
+            copy("pms%d" % t, "v" if "pms%d" % t in sum(VSEQ, []) else "s", [last], T.z[:, t, r], pm[:, 0:128])
+            order["k"].append(send("sz%d" % t, ["pms%d" % t], "a%d" % t, T.z[:, t, r], "n%d" % t))
         else:
-            V("z%d" % t, ["n%dm" % t], "tr", T.yo[:, k, :], pm[:, 0:128])
+            V("z%d" % t, [last], "tr", T.yo[:, k, :], pm[:, 0:128])
             order["y"] += [store("y%d" % t, "z%d" % t, 0, 2)] if span[k] == 4 else [store("y%d%s" % (t, "ab"[h]), "z%d" % t, h, 1) for h in range(2)]
-        for x in PSEQ.get(t, ["m%d" % (t - 1), "e%d" % (t + 1), "a%d" % (t + 1), "n%dm" % (t - 1), "o%d" % (t + 2)]):
-            order["p"] += chains.get(x, [x] if x != "o%d" % NT else [])
 
     total = {}
     for q in order:

from concourse.bass import DstId, RemoteDMATransfer
from concourse.mybir import AluOpType, ActivationFunctionType

OP = AluOpType
COPY = ActivationFunctionType.Copy
N = 4
NBLK = 4
NT = 3 * NBLK
GROUPS = [([0], "v"), ([1], "s"), ([2, 3], "s")]
TQ = 8
NEAR = 8
START = {
    "k": ["jp", "pf", "jc", "sg", "sb0", "sb1", "jm", "sb2", "big", "wz0"],
    "v": ["col0", "mz0", "ident", "og0", "xb00", "xb01", "wf", "xt0", "xb10", "xb11", "oh0", "oh1", "xt1", "zb0", "xb20", "xb21", "oh2", "oh3", "xt2",
          "oh4", "oh5", "col1", "col2", "msk", "off0"],
    "s": ["gi", "gd", "wi", "mz1", "one", "id4", "zb1", "wm0", "zb2", "wm1", "wm2"],
    "p": ["po", "pl0", "pl1", "pwm0", "pl2", "pwm1", "pwm2", "o0", "e0", "a0"],
}
VSEQ = [
    [54, "off1", "og1"],
    [52, "off2", "og2", "pms0"],
    [68, "pms1"],
    [66, "pms2", "off4"],
    [54, "pms3", "off5"],
    [54, "pms4", "off6"],
    [54, "pms5", "off7"],
    [56, "pms6", "off8"],
    [56, "pms7", "off9"],
    [62, "off10", "z8"],
    [58, "off11", "z9"],
]
SSEQ = [[74], [76], ["wc1", 60], ["wc2", 62], [74], [74], [74], [72], [72], [66], [70]]
PSEQ = [
    ["o1", "e1", "a1", "o2", "e2"],
    ["a2", "pw10", 5, "pw11", 5, "pw12", 6, "pw13"],
    ["pw20", 5, "pw21", 5, "pw22", 6, "pw23", "o4", "h2_1"],
    [16, "e4", "a4", "o5", "h3_1"],
    [16, "e5", "a5", "o6", "h4_1"],
    [16, "e6", "a6", "o7", "h5_1"],
    [16, "e7", "a7", "o8", "h6_1"],
    [16, "e8", "a8", "o9", "h7_1"],
    [16, "e9", "a9", "o10"],
    [9, "e10", "a10", 7, "o11"],
    [10, "e11", "a11", 6],
    [16, "m11a", "m11b"],
]
LAST = [("v", 0, 32), ("s", 32, 32), ("v", 64, 30), ("s", 94, 34)]

SCRATCH = {
    "xi": ("sbuf", [128, 2, 256], "int32"),
    "gi": ("sbuf", [128, 3], "int32"),
    "gd": ("dram", [4, 128, 3], "int32"),
    "gg": ("sbuf", [128, 3], "int32"),
    "wi": ("sbuf", [128, 6], "int32"),
    "tab": ("sbuf", [128, 2, 4096], "bfloat16"),
    "tab3": ("sbuf", [128, 8192], "bfloat16"),
    "jc": ("sbuf", [128, 128], "bfloat16"),
    "jp": ("sbuf", [128, 128], "bfloat16"),
    "jm": ("sbuf", [128, 128], "bfloat16"),
    "pf": ("sbuf", [128, 1], "float32"),
    "col": ("sbuf", [128, 3, 8], "uint16"),
    "ident": ("sbuf", [128, 128], "bfloat16"),
    "id4": ("sbuf", [128, 4, 2, 16], "bfloat16"),
    "big": ("sbuf", [128, 4, 2, 16], "bfloat16"),
    "msk": ("sbuf", [128, 16, 144], "bfloat16"),
    "og": ("sbuf", [128, 3, 128], "bfloat16"),
    "one": ("sbuf", [128, 128], "bfloat16"),
    "wf": ("sbuf", [128, 6], "float32"),
    "oh": ("sbuf", [128, 6, 128], "bfloat16"),
    "wr": ("sbuf", [128, 4, 128], "bfloat16"),
    "wm": ("sbuf", [128, 3, 128], "bfloat16"),
    "wc": ("sbuf", [128, 4, 128], "bfloat16"),
    "wz": ("sbuf", [128, 8, 9, 16], "bfloat16"),
    "xb": ("sbuf", [128, 16, 2, 16], "bfloat16"),
    "xt": ("sbuf", [128, NBLK, 64, 2], "bfloat16"),
    "z": ("sbuf", [128, 8, 4, 4, 2, 16], "bfloat16"),
    "off": ("sbuf", [128, NT, 128], "uint16"),
    "gt": ("sbuf", [128, NT, 2048], "bfloat16"),
    "yo": ("sbuf", [128, NBLK, 128], "float32"),
    "pm0": ("psum", [128, 512], "float32"),
    "pm1": ("psum", [128, 512], "float32"),
    "pa0": ("psum", [128, 16, 2, 16], "float32"),
    "pa1": ("psum", [128, 16, 2, 16], "float32"),
    "pw": ("psum", [128, 512], "float32"),
    "pl": ("psum", [128, 512], "float32"),
    "pv": ("psum", [128, 512], "float32"),
}
for _i in range(3):
    SCRATCH["zb%d" % _i] = ("sbuf", [128, 4, 128 * len(GROUPS[_i][0])], "bfloat16")
SEMAPHORES = ["v", "p", "s", "k", "gs", "gd", "gg", "ga", "wl", "yd", "loc", "t0"] + [_s + str(_i) for _i in range(3) for _s in "xbc"]
SEMAPHORES += ["t%d%d" % (_l, _q) for _l in (1, 2) for _q in range(8)] + [_s + str(_t) for _t in range(8) for _s in "an"]


def rank_program(g, core, T, topo):
    r = T.rank_of(core)
    if r is None:
        return
    queues = {"v": g.vector, "p": g.tensor, "s": g.scalar, "k": g, "y": g.sync}
    steps = {}

    def step(name, q, deps, emit, sem=None, n=1):
        steps[name] = {"q": q, "deps": [d for d in deps if d], "emit": emit, "sem": sem or q, "n": n}
        return name

    def V(name, deps, call, *a):
        f = {"copy": g.vector.tensor_copy, "ts": g.vector.tensor_scalar, "tt": g.vector.tensor_tensor, "tr": g.vector.transpose,
             "set": g.vector.memset}[call]
        return step(name, "v", deps, lambda: f(*a))

    def S(name, deps, out, in_):
        return step(name, "s", deps, lambda: g.scalar.activation(out, in_, COPY))

    def copy(name, q, deps, out, in_):
        return V(name, deps, "copy", out, in_) if q == "v" else S(name, deps, out, in_)

    def MM(name, deps, calls):
        def emit():
            for c in calls:
                x = g.tensor.matmul(*c)
            return x
        return step(name, "p", deps, emit)

    def dma(name, q, deps, out, in_, sem):
        return step(name, q, deps, lambda: queues[q].dma_start(out, in_), sem, 16)

    def iota(name, out, pattern, cm):
        return step(name, "k", [], lambda: g.iota(out, pattern, 0, cm, allow_small_or_imprecise_dtypes=True))

    dst = {d: T.cores[(r + d) % N] for d in (1, 2, 3)}
    far = [d for d in dst if topo.chip(dst[d]) != topo.chip(core)]
    near = [d for d in dst if d not in far]
    use = {}
    farset = set()
    for j, d in enumerate(far):
        en = topo.engines(core, dst[d])
        farset |= set(en)
        w = len(en) // len(far)
        use[d] = en[j * w:j * w + w]
    for d in near:
        en = [x for x in topo.engines(core, dst[d]) if x not in farset]
        use[d] = en[::len(en) // NEAR]
    total_eng = sum(len(use[d]) for d in dst)
    landed = {}

    def send(name, deps, sem, part, early=None):
        def emit():
            tr = []
            for d in far + near:
                rid, pid, _ = topo.addr(dst[d])
                tr.append(RemoteDMATransfer(dst_ids=[DstId(rid=rid, pnc=pid)], dma_engine_mask=sum(1 << x for x in use[d]),
                                            remote_sem=T.sem[early if early and d in near else sem], src=part, dst=part))
            g.remote_dma_fused(tr, local_sem=T.sem.loc)
            return None
        if early:
            landed[early] = {"sem": early, "tok": NEAR}
        return step(name, "k", deps, emit, sem, total_eng - (NEAR if early else 0))

    dma("gd", "s", [], T.gd[r], T.give[:], "gd")
    dma("gi", "s", [], T.gi[:], T.give[:], "gs")
    dma("wi", "s", [], T.wi[:], T.wires[:], "wl")
    xs, base, span = [], {}, {}
    for i, (bl, _) in enumerate(GROUPS):
        lo, hi = bl[0], bl[-1] + 1
        xs += [dma("x%d%d" % (i, c), "y", [], T.xi[:, c, 64 * lo:64 * hi], T.x[64 * c:64 * c + 64, 128 * lo:128 * hi], "x%d" % i) for c in range(2)]
        for k in bl:
            base[k], span[k] = 4 * (lo + k), 4 * len(bl)
    t0 = [dma("t0%d" % h, "y", [], T.tab[16 * h:16 * h + 32, 0, :], T.tb[h:h + 2, 0:65536], "t0") for h in range(0, 8, 2)]
    later = []
    for h in range(8):
        later.append(dma("t1%d" % h, "y", ["sb0" if h < TQ else later[-TQ]], T.tab[16 * h:16 * h + 16, 1, :], T.tb[h:h + 1, 65536:131072], "t1%d" % (h % TQ)))
    for h in range(16):
        k, a, c = h // 4, h // 2 % 2, h % 2
        later.append(dma("t2%d" % h, "y", [later[-TQ]], T.tab3[32 * k + 16 * a:32 * k + 16 * a + 16, 4096 * c:4096 * c + 4096],
                         T.tb[2 * k + c:2 * k + c + 1, 131072:196608], "t2%d" % (h % TQ)))
    tabs = [t0, later[:8], later[8:]]
    window = [T.tab[:, 0, :], T.tab[:, 1, :], T.tab3[:]]

    iota("jp", T.jp[:], [[16, 4], [64, 2], [1, 16]], 0)
    iota("pf", T.pf[:], [[0, 1]], 1)
    iota("jc", T.jc[:], [[1, 128]], 0)
    iota("jm", T.jm[:], [[1, 16], [16, 8]], 0)
    iota("wz0", T.wz[:, :, 0:9:2, :], [[0, 640]], 0)
    iota("big", T.big[:], [[0, 4], [4096, 2], [0, 16]], 0)
    for l in range(3):
        V("col%d" % l, [], "set", T.col[:, l, :], l)
    V("ident", ["jc", "pf"], "ts", T.ident[:], T.jc[:], T.pf[:], None, OP.is_equal)
    S("id4", ["ident"], T.id4[:], T.ident[:])
    V("mz0", [], "set", T.msk[:, 0:10, :], 0.0)
    S("mz1", ["mz0"], T.msk[:, 10:16, :], T.msk[:, 0:6, :])
    V("msk", ["mz0", "mz1", "jm", "pf"], "ts", T.msk[:, :, 15:143:16], T.jm[:], T.pf[:], None, OP.is_equal)

    send("sg", ["gd"], "ga", T.gd[r])
    V("og0", ["gi", "jp", "col0"], "tt", T.og[:, 0, :], T.gi[:].indirect(T.col[:, 0, :]), T.jp[:], OP.is_equal)
    MM("po", ["og0", "ident"], [(T.pw[:, 0:128], T.og[:, 0, :], T.ident[:], True, True)])
    S("one", ["po"], T.one[:], T.pw[:, 0:128])
    for i, (bl, q) in enumerate(GROUPS):
        lo, hi = bl[0], bl[-1] + 1
        bank, zb = [T.pl, T.pv, T.pw][i], T["zb%d" % i]
        for c in range(2):
            V("xb%d%d" % (i, c), ["x%d0" % i, "x%d1" % i], "copy", T.xb[:, 4 * lo:4 * hi, c, :], T.xi[:, c, 64 * lo:64 * hi])
        V("xt%d" % i, ["xb%d0" % i, "xb%d1" % i], "tr", T.xt[:, lo:hi], T.xb[:, 4 * lo:4 * hi])
        MM("pl%d" % i, ["xt%d" % i, "one"], [(bank[:, 128 * j + 64 * a:128 * j + 64 * a + 64], T.one[:], T.xt[:, k, :, a], True, True)
                                             for j, k in enumerate(bl) for a in range(2)])
        copy("zb%d" % i, q, ["pl%d" % i], zb[:, r, :], bank[:, 0:128 * len(bl)])
        send("sb%d" % i, ["zb%d" % i], "b%d" % i, zb[:, r, :], "c%d" % i)

    V("wf", ["wi"], "copy", T.wf[:], T.wi[:])
    for l in range(3):
        V("oh%d" % (2 * l), ["wf", "jc"], "ts", T.oh[:, 2 * l, :], T.jc[:], T.wf[:, 2 * l:2 * l + 1], 64.0, OP.is_equal, OP.mult)
        V("oh%d" % (2 * l + 1), ["wf", "jc"], "ts", T.oh[:, 2 * l + 1, :], T.jc[:], T.wf[:, 2 * l + 1:2 * l + 2], None, OP.is_equal)
    mine = slice(32 * r, 32 * r + 32)
    MM("pwm0", ["oh0", "oh1", "ident"], [(T.pm1[mine, 128 * q:128 * q + 128], T.oh[:, i, 32 * q:32 * q + 32], T.ident[:], i == 0, i == 1)
                                         for q in range(N) for i in range(2)])
    S("wm0", ["pwm0"], T.wr[mine], T.pm1[mine, :])
    MM("pwm1", ["oh2", "oh3", "ident"], [(T.pm0[:, 0:128], T.oh[:, 2 + i, :], T.ident[:], i == 0, i == 1) for i in range(2)])
    S("wm1", ["pwm1"], T.wm[:, 1, :], T.pm0[:, 0:128])
    MM("pwm2", ["oh4", "oh5", "id4", "zb0"], [(T.pl[:, 64 * c:64 * c + 64], T.oh[:, 4 + i, :], T.id4[:, :, c, :], i == 0, i == 1) for c in range(2) for i in range(2)])
    S("wm2", ["pwm2"], T.wm[:, 2, :], T.pl[:, 0:128])
    dma("gg", "y", ["sg", "gd"], T.gg[:], T.gd[:, 32 * r:32 * r + 32, :], "gg")
    for l in (1, 2):
        V("og%d" % l, ["gg", "jc", "col%d" % l], "tt", T.og[:, l, :], T.gg[:].indirect(T.col[:, l, :]), T.jc[:], OP.is_equal)
        a = "zb2" if l == 1 else "zb1"
        for q in range(N):
            out = (T.pw if l == 1 else T.pv)[:, 128 * q:128 * q + 128]
            a = MM("pw%d%d" % (l, q), ["wm%d" % l, "og%d" % l, a], [(out, T.og[32 * q:32 * q + 32, l, :], T.wm[32 * q:32 * q + 32, l, :], True, True)])
    S("wc1", ["pw13"], T.wc[:], T.pw[:])
    S("wc2", ["pw23", "wz0"], T.wz[:, :, 1:9:2, :], T.pv[:])

    ranks = [(r + d) % N for d in [0] + near + far]
    order = {q: list(START.get(q, [])) for q in queues}
    order["y"] = xs + t0 + ["gg"] + later
    for t in range(NT):
        l, k = divmod(t, NBLK)
        u = 0
        for x in PSEQ[t]:
            order["p"].append("m%d_%d" % (t - 1, u) if isinstance(x, int) else x)
            u += x if isinstance(x, int) else 0
        pa, pm = T["pa%d" % (t % 2)], T["pm%d" % (t % 2)]
        n = 2 if t == 2 else 1
        if l == 0:
            calls = [(pa[:, 0:4 * n], T.wr[mine, q, :], T["zb%d" % min(t, 2)][mine, q, :], q == ranks[0], q == ranks[-1]) for q in ranks]
            need = [["zb%d" % t, "wm0"], "c%d" % t, "sb%d" % t]
        elif l == 1:
            calls = [(pa[:, 0:4], T.wc[:, q, :], T.z[:, t - 4, q], q == ranks[0], q == ranks[-1]) for q in ranks]
        else:
            calls = [(pa[:, 0:4], T.ident[:], T.big[:], True, False)]
            calls += [(pa[:, 0:4, c, :], T.wz[:, 2 * q + c, 1 - a:9 - a, :], T.z[:, t - 4, q, :, a, :], False, q == ranks[-1] and a == 1 and c == 1)
                      for q in ranks for c in range(2) for a in range(2)]
        if l:
            need = [["pms%d" % (t - 4), "wc%d" % l, "big"], "n%d" % (t - 4), "sz%d" % (t - 4)]
        if t != 3:
            w = len(calls) // N
            free = {0: None, 1: None, 5: "off1"}.get(t, "off%d" % (t - 2))
            MM("o%d" % t, need[0] + [free], calls[:-3 * w])
            MM("e%d" % t, [need[1]], calls[-3 * w:-len(far) * w])
            MM("a%d" % t, [need[2]], calls[-len(far) * w:])
            V("off%d" % t, ["a%d" % t], "copy", T.off[:, t:t + n, :], pa[:, 0:4 * n])

        def gather(name, q, b, n):
            return copy(name, q, ["off%d" % (2 if t == 3 else t)] + tabs[l], T.gt[:, t, 16 * b:16 * b + 16 * n], window[l].indirect(T.off[:, t, b:b + n]))

        def merge(name, deps, out, lo, w, units=range(16)):
            return MM(name, deps + ["msk"], [(out, T.msk[:, u, 15 - u:143 - u], T.gt[:, t, 16 * lo + u:16 * lo + 16 * w:16], u == 0, u == 15)
                                             for u in units])

        def store(name, dep, h, n):
            c0 = 16 * (base[k] + h * span[k])
            return dma(name, "y", [dep], T.y[:, c0:c0 + 64 * n], T.yo[:, k, 64 * h:64 * h + 64 * n], "yd")

        held = ["wm1", "wm0"][t] if t < 2 else ("pms%d" if t < 10 else "z%d") % (t - 2)
        if t == NT - 1:
            gs = [gather("g%d_%d" % (t, j), q, b, n) for j, (q, b, n) in enumerate(LAST)]
            merge("m11a", gs[0:2] + [held], pm[:, 0:64], 0, 64)
            merge("m11b", gs[2:4] + ["wm2"], T.pl[:, 0:64], 64, 64)
            V("z11a", ["m11a"], "tr", T.yo[:, k, 0:64], pm[:, 0:64])
            V("z11b", ["m11b"], "tr", T.yo[:, k, 64:128], T.pl[:, 0:64])
            order["v"] += [gs[0], gs[2], "z10", "z11a", "z11b"]
            order["s"] += [gs[1], gs[3]]
            order["y"] += [store("y11a", "z11a", 0, 1), store("y11b", "z11b", 1, 1)]
            continue
        seq = {"v": VSEQ[t], "s": SSEQ[t]}
        calls = sorted((j, q != "v", q, n) for q in seq for j, n in enumerate([x for x in seq[q] if isinstance(x, int)]))
        gs, b = [], 0
        for j, _, q, n in calls:
            gs.append(gather("g%d_%s%d" % (t, q, j), q, b, n))
            b += n
        assert b == 128
        for q in seq:
            j = 0
            for x in seq[q]:
                order[q].append("g%d_%s%d" % (t, q, j) if isinstance(x, int) else x)
                j += isinstance(x, int)
        lo, u = 0, 0
        for n in (1, 2):
            if "h%d_%d" % (t, n) in PSEQ[t] + PSEQ[t + 1]:
                lo = sum(c[3] for c in calls[:n])
                merge("h%d_%d" % (t, n), gs[:n] + [held], pm[:, 0:lo], 0, lo)
        for n in PSEQ[t + 1]:
            if isinstance(n, int):
                last = merge("m%d_%d" % (t, u), gs + [held], pm[:, lo:128], lo, 128 - lo, range(u, u + n))
                u += n
        if l < 2:
            copy("pms%d" % t, "v" if "pms%d" % t in sum(VSEQ, []) else "s", [last], T.z[:, t, r], pm[:, 0:128])
            order["k"].append(send("sz%d" % t, ["pms%d" % t], "a%d" % t, T.z[:, t, r], "n%d" % t))
        else:
            V("z%d" % t, [last], "tr", T.yo[:, k, :], pm[:, 0:128])
            order["y"] += [store("y%d" % t, "z%d" % t, 0, 2)] if span[k] == 4 else [store("y%d%s" % (t, "ab"[h]), "z%d" % t, h, 1) for h in range(2)]

    total = {}
    for q in order:
        for name in order[q]:
            n = steps[name]
            total[n["sem"]] = n["tok"] = total.get(n["sem"], 0) + n["n"]
    assert sum(len(o) for o in order.values()) == len(steps)
    steps.update(landed)
    sent = 0
    seen = {}
    for q in order:
        waited = {}
        for name in order[q]:
            n = steps[name]
            need = {}
            for d in n["deps"]:
                s = steps[d]["sem"]
                need[s] = max(need.get(s, 0), steps[d]["tok"])
            for s in sorted(need):
                if waited.get(s, 0) < need[s]:
                    queues[q].wait_ge(T.sem[s], need[s])
                    waited[s] = need[s]
                    seen[s] = max(seen.get(s, 0), need[s])
            x = n["emit"]()
            if x is None:
                sent += total_eng
            else:
                x.then_inc(T.sem[n["sem"]], n["n"])
    g.wait_ge(T.sem.loc, sent)
    for s in sorted(total):
        if seen.get(s, 0) < total[s]:
            g.sync.wait_ge(T.sem[s], total[s])
